import numpy as np, ml_dtypes
CORES = [1,5,17,21,33,37,49,53]
N = 8
import mx_ref
BF = ml_dtypes.bfloat16
def gentries(a):
    return np.ascontiguousarray(a.reshape(8, 16, -1).transpose(0, 2, 1)).reshape(8, -1)
def gtable(e):
    e = np.asarray(e); return np.ascontiguousarray(e.reshape(8, -1, 16).transpose(0, 2, 1)).reshape(128, -1).astype(np.int32)
def gcols(t, e):
    v = np.concatenate([t.reshape(8, 16, -1, 4), np.zeros((8, 16, 1, 4), BF)], axis=2)
    return np.ascontiguousarray(np.stack([v[g][:, e[g]] for g in range(8)])).reshape(128, -1)
def gpick(z, e):
    return np.concatenate([z[16 * g:16 * g + 16][:, e[g]] for g in range(8)])
def tile(rs):
    return np.stack(rs, axis=2).reshape(128, -1).astype(BF)
def pick(q, e):
    c = np.concatenate([q[0].reshape(128, -1, 4), np.zeros((128, 1, 4), np.uint8)], axis=1); s = np.concatenate([q[1], np.ones((16, 1), np.uint8)], axis=1)
    return (np.ascontiguousarray(c[:, e].reshape(128, -1)), np.ascontiguousarray(s[:, e]))
def join(*qs):
    return (np.concatenate([q[0] for q in qs], axis=1), np.concatenate([q[1] for q in qs], axis=1))
def put(q, e, v):
    c, s = q[0].reshape(128, -1, 4).copy(), q[1].copy(); c[:, e] = v[0].reshape(128, -1, 4); s[:, e] = v[1]
    return (c.reshape(128, -1), s)
def pk(c, s):
    return (np.ascontiguousarray(c), mx_ref.live(s))
def emit(q):
    return q[0], q[1]
def packed(v, rng):
    q = [mx_ref.quantize(np.ascontiguousarray(v[r])) for r in range(N)]
    return np.stack([a for a, b in q]), np.stack([mx_ref.plane(b, rng) for a, b in q])
def values_of_codes():
    e, c = np.zeros((128, 128, 4), np.float32), np.zeros((128, 2, 4), np.uint8)
    e[np.arange(128), np.arange(128), 0] = 1
    c[:127, :, 0] = np.arange(256).reshape(2, 128).T[:127]
    return mx_ref.matmul(mx_ref.quantize(e.reshape(128, 512).astype(BF)), (c.reshape(128, 8), np.full((16, 2), 127, np.uint8))).T.reshape(-1).astype(np.float64)
CODE_VALUE, SCALE_VALUE = values_of_codes(), 2.0 ** (np.arange(256) - 127.0)
def decode(q):
    return (CODE_VALUE[q[0]].reshape(16, 8, -1, 4) * SCALE_VALUE[q[1]][:, None, :, None] + 0.0).reshape(128, -1).astype(np.float32)
def f(rng, *shape):
    return mx_ref.flush((rng.standard_normal(shape, dtype=np.float32) * np.exp2(rng.integers(-2, 3, shape[:-1] + (1,)))).astype(BF))
def wide(rng, *shape, cols=0):
    v = rng.standard_normal(shape, dtype=np.float32) * np.exp2(rng.integers(-12, 13, shape)).astype(np.float32)
    if cols: v *= np.repeat(np.exp2(rng.integers(-cols, cols + 1, shape[:-2] + (1, shape[-1] // 4))) * (rng.random(shape[:-2] + (1, shape[-1] // 4)) > 0.0625), 4, axis=-1).astype(np.float32)
    return mx_ref.flush(v.astype(BF))
C = 256
MASK = [1, 2, 4]
PARITY = np.array([(r ^ (r >> 1) ^ (r >> 2)) & 1 for r in range(N)])
def numbers_of(rng):
    return {"x": np.array(f(rng, N, 128, 4 * C)), "u": np.array(f(rng, N, 128, 512)), "v": np.array(f(rng, N, 128, 512))}
def stored(k):
    return {"fl": np.stack([gtable(k[r]) for r in range(N)])}
def lists(rng):
    return stored(rng.permuted(np.tile(np.arange(C), (N, 8, 1)), axis=2))
def layers(rng):
    return np.array(f(rng, N, 128, 2048)).reshape(N, 8, 16, 4, 8, 16, 4)
def weights(rng, w):
    c, p = packed(np.ascontiguousarray(w).reshape(N, 128, 2048), rng)
    return {"wc": c, "ws": p}
def setup_inputs(rng):
    return {**numbers_of(rng), **lists(rng), **weights(rng, layers(rng))}
def setup_inputs_long(rng):
    d = numbers_of(rng)
    kind = rng.permutation(8)
    s = np.tile(rng.choice([-1.0, 1.0], (8, C)), (N, 1, 1))
    k = np.zeros((N, 8, C), np.int64)
    for g in range(8):
        c, p = rng.permutation(C), int(rng.integers(C))
        if kind[g] == 0: c, p = np.arange(C), C - N // 2
        if kind[g] == 1: c = np.arange(C)[::-1]
        k[:, g, c] = np.roll(c, -1)
        for r in range(N):
            if kind[g] in (0, 1, 3, 4): s[r, g, c[(p + r) % C]] *= -1
            if kind[g] == 2 and PARITY[r]: s[r, g, c[p]] *= -1
            if kind[g] == 6 and PARITY[r]: s[r, g] *= -1
            if kind[g] == 7:
                s[r, g] = rng.choice([-1.0, 1.0], C)
                k[r, g] = np.arange(C)
    x = d["x"].reshape(N, 8, 16, C, 4)
    x[:, :, 0] = 0
    x[:, :, 0, :, 0] = s.astype(np.float32).astype(BF)
    u = d["u"].reshape(N, 128, 128, 4)
    u[:, :, ::16] = 0
    for h in range(0, 128, 16): u[:, h, h, 0] = 1
    w = layers(rng)
    w[:, :, :, :, :, 0] = 0
    return {"x": x.reshape(N, 128, 4 * C), "u": u.reshape(N, 128, 512), "v": d["v"], **stored(k), **weights(rng, w)}
def setup_inputs_near(rng):
    d = numbers_of(rng)
    o, e = rng.permutation(N) % 2, rng.permutation(N)
    k = np.where(o == 0, 2.0 ** -27, 1.0)
    m = np.where(o == 0, 2.0 ** -30, 1.0)
    s = rng.integers(-1, 2, (N, 8, C))
    s[e[0]] = 0
    s[e[1]] = 1
    x = d["x"].astype(np.float32).reshape(N, 8, 16, C, 4)
    x[o == 0] = 0
    x[:, :, :3] = 0
    x[:, :, 8:] = 0
    x[:, :, 0, :, 0] = np.where(s == 0, 1.0, 1.125 * s) * k[:, None, None]
    x[:, :, 1, :, 0] = np.where(s == 0, -1.125, -1.25 * s) * k[:, None, None]
    x[:, :, 3, :, 0] = k[:, None, None]
    x[:, :, 8, :, 0] = rng.choice([-1.0, 1.0], (N, 8, C)) * 2.0 ** -30
    x[:, :, 9, :, 0] = 2.0 ** -26
    for r in range(N):
        for g in rng.permutation(8)[:4]: x[r, g, 0, rng.integers(C), 0] = 2.0 ** 30 * rng.choice([-1.0, 1.0])
    u = d["u"].reshape(N, 128, 128, 4)
    u[:, :, ::16] = 0
    for h in range(0, 128, 16):
        u[:, h, h, 0] = (1.125 * m).astype(np.float32).astype(BF)
        u[:, h + 1, h, 0] = m.astype(np.float32).astype(BF)
        u[:, h + 2, h, 0] = m.astype(np.float32).astype(BF)
    w = layers(rng)
    w[:, :, :, :, :, :10] = 0
    for g in range(8): w[:, g, 8, 0, g, 2, 0] = 2.0 ** -7
    return {"x": x.reshape(N, 128, 4 * C).astype(BF), "u": u.reshape(N, 128, 512), "v": d["v"], **lists(rng), **weights(rng, w)}
def setup_inputs_odd(rng):
    d = numbers_of(rng)
    e = (PARITY[:, None] + rng.permutation(8)) % 2
    a = 1.0 + (2 * rng.integers(0, 64, (N, 8, 16, C, 4)) + 1) * 2.0 ** -7
    x = np.zeros((N, 8, 16, C, 4))
    x[:, :, :8] = a[:, :, :8] * np.exp2(-rng.integers(0, 7, (N, 8, 8, C, 4)).astype(np.float64)) * rng.choice([-1.0, 1.0], (N, 8, 8, C, 4))
    x[:, :, 0] = 0
    x[:, :, 0, :, 0] = 1.96875 * 2.0 ** 8 * rng.choice([-1.0, 1.0], (N, 8, C))
    x[:, :, 8:] = np.where(e[:, :, None, None, None] == 0, a[:, :, 8:] * np.exp2(12.0 - rng.integers(8, 15, (N, 8, 8, C, 4))), 0.0)
    x[:, :, 8, :, 0] = (np.where(e == 0, -1.0, 1.0) * 1.96875 * 2.0 ** 12)[:, :, None]
    u = d["u"].reshape(N, 128, 128, 4)
    u[:, 8::16, ::16] = 0
    w = layers(rng)
    for i in (0, 8):
        w[:, :, i] = 0
        w[:, :, :, :, :, i] = 0
    for g in rng.permutation(8)[:4]:
        x[:, g, :3] = 0
        x[:, g, 0, :, 0] = 1.96875 * 2.0 ** 8
        x[:, g, 1, :, 0] = (8 + rng.integers(-1, 2, (N, C))) * 2.0 ** -8
        x[:, g, 2, :, 0] = -2.0 ** -5
        x[:, g, 8:] = 0
        x[:, g, 8, :, 0] = 1.96875 * 2.0 ** 12
        x[:, g, 9] = rng.integers(1, 16, (N, C, 4)) * 2.0 ** -4
        u[:, 16 * g, ::16] = 0
        u[:, :, 16 * g] = 0
        u[:, 16 * g + 1:16 * g + 3, 16 * g, 0] = 1
        w[:, :, :, :, g] = 0
        for i in (0, 8): w[:, g, i, 0, g, i, 0] = -0.5
        for b in range(4): w[:, g, 9, b, g, 10, b] = 256.0
    return {"x": x.astype(np.float32).reshape(N, 128, 4 * C).astype(BF), "u": u.reshape(N, 128, 512), "v": d["v"], **lists(rng), **weights(rng, w)}
def setup_inputs_ends(rng):
    d = numbers_of(rng)
    x = np.zeros((N, 8, 16, C, 4))
    u = d["u"].astype(np.float32).reshape(N, 128, 128, 4)
    v = np.zeros((N, 128, 512))
    w = np.zeros((N, 128, 4, 128, 4), np.float32)
    o = rng.permutation(N) % 4
    third, others = np.flatnonzero(o == 2), np.flatnonzero(o != 2)
    if len(third) == 2 and third[0] ^ third[1] == MASK[0]:
        p = rng.choice(others)
        o[third[1]] = o[p]
        o[p] = 2
    i, at = np.arange(128), np.arange(C)
    k = np.zeros((N, 8, C), np.int64)
    for r in range(N):
        h = rng.permutation(8)
        c = np.where(h < 2, 0.0, h % 2 * 2.0 - 1.0)[None, :, None]
        low = -(0.9 + 0.1 * rng.random((8, 16, C, 4))) * 2.0 ** 30
        if o[r] == 0: x[r] = low
        if o[r] == 1: x[r] = low * rng.choice([-1.0, 1.0], C)[:, None]
        if o[r] == 2: x[r] = -(1.0 + 0.125 * rng.integers(0, 8, (8, 16, C, 4))) * 2.0 ** -30
        if o[r] == 3: x[r] = d["x"][r].astype(np.float32).reshape(8, 16, C, 4)[:, :, :1]
        if o[r] < 2:
            u[r, :, ::16] = c * (0.9 + 0.1 * rng.random((128, 8, 4))) * 2.0 ** 30
            v[r] = rng.choice([-1.0, 1.0], (128, 512)) * (0.9 + 0.1 * rng.random((128, 512))) * 2.0 ** 30
        else: v[r] = rng.choice([-1.0, 1.0], (128, 512)) * (1.0 + 0.125 * rng.integers(0, 8, (128, 512))) * 2.0 ** -30
        if o[r] == 2: u[r, :, ::16] = c * (1.0 + 0.125 * rng.integers(0, 8, (128, 8, 4))) * 2.0 ** -30
        if o[r] == 3: u[r, :, ::16] *= np.abs(c).astype(np.float32)
        t = np.array([4.0, 8.0, 16.0])[rng.permutation(8) % 3]
        if o[r] == 2: t[:] = 2.0 ** -8
        if o[r] == 3: t[:] = 2.0 ** 5
        for b in range(4): w[r, i, b, i, b] = t[i // 16]
        for g, n in enumerate(rng.permutation(8) % 5): k[r, g] = [at, at[::-1], np.roll(at, -1), at ^ 1, rng.permutation(C)][n]
    return {"x": x.astype(np.float32).reshape(N, 128, 4 * C).astype(BF), "u": u.reshape(N, 128, 512).astype(BF), "v": v.astype(np.float32).astype(BF), **stored(k), **weights(rng, w.astype(BF))}
def setup_inputs_spread(rng):
    d = numbers_of(rng)
    w = layers(rng).reshape(N, 128, 4, 128, 4)
    i, r = np.arange(128), int(rng.integers(N))
    for b in range(4): w[r, i, b, i, b] = 256.0
    return {"x": wide(rng, N, 128, 4 * C, cols=6), "u": d["u"], "v": d["v"], **lists(rng), **weights(rng, w)}
def check_inputs(d):
    b = []
    for k in ("x", "u", "v"):
        a = np.abs(d[k].astype(np.float32))
        if not (np.isfinite(a).all() and ((a == 0) | (a >= 2.0 ** -30) & (a <= 2.0 ** 30)).all()): b.append("a value of " + k)
    none, least, most = [emit(mx_ref.quantize(np.full((128, 16), k, np.float32).astype(BF)))[1][0, 0] for k in (0.0, 2.0 ** -8, 2.0 ** 8)]
    for r in range(N):
        if not (np.sort(gentries(d["fl"][r]), axis=1) == np.arange(C)).all(): b.append("fl: a group's entries are no permutation")
        if ((d["wc"][r] == 0x7F) | (d["wc"][r] == 0xFF)).any(): b.append("wc: a code that is no number")
        s = mx_ref.live(d["ws"][r])
        if ((s != none) & ((s < least) | (s > most))).any(): b.append("ws: a scale out of range")
        if (((d["wc"][r].reshape(16, 8, 512, 4) & 0x7F) != 0) & (s == none)[:, None, :, None]).any(): b.append("wc: a code other than zero under the scale of zeros")
    return b
def returns(e, gate):
    at = np.tile(np.arange(C), (8, 1))
    step = np.where(gate, at, e)
    a = e
    for i in range(C): a = np.take_along_axis(step, a, axis=1)
    return np.where(gate, a, at)
def reference(x, u, v, fl, wc, ws):
    half = np.float32(0.5)
    qu = [mx_ref.quantize(u[r]) for r in range(N)]
    lay = [pk(wc[r], ws[r]) for r in range(N)]
    own = [gentries(fl[r]).astype(np.int64) for r in range(N)]
    now = [x[r] for r in range(N)]
    for m in MASK:
        q = [mx_ref.quantize(now[r]) for r in range(N)]
        t = [decode(q[r]) for r in range(N)]
        bit = [mx_ref.matmul(qu[r], q[r])[::16] > 0 for r in range(N)]
        made, new = [], []
        for r in range(N):
            d = r ^ m
            a = returns(own[d], bit[r] != bit[d])
            n = np.take_along_axis(own[r], a, axis=1)
            z = (gcols(t[r].astype(BF), n).astype(np.float32) + gcols(t[d].astype(BF), a).astype(np.float32)) * half
            qz = mx_ref.quantize(z.astype(BF))
            back = np.argsort(n, axis=1)
            p = [mx_ref.matmul(pick(lay[r], np.arange(128 * b, 128 * b + 128)), qz) * np.float32(0.03125) for b in range(4)]
            made.append(tile([(t[r][:, b::4] + gpick(p[b], back)) * half for b in range(4)]))
            new.append(n)
        now, own = made, new
    y, ln = np.zeros((N, 128, C), np.float32), np.zeros((N, 8, C), np.float32)
    oc, osc = np.zeros((N, 128, 4 * C), np.uint8), np.zeros((N, 16, C), np.uint8)
    for r in range(N):
        q = mx_ref.quantize(now[r])
        y[r] = mx_ref.matmul(mx_ref.quantize(v[r]), q)
        ln[r] = own[r]
        oc[r], osc[r] = emit(q)
    return {"y": y, "ln": ln, "oc": oc, "osc": osc}

@@ -1,0 +1,307 @@
+from concourse.bass import IndirectOffsetOnAxis
+from concourse.mybir import dt, AluOpType, ActivationFunctionType
+
+C = 256
+ROUNDS = (1, 2, 4)
+COPY = ActivationFunctionType.Copy
+LIFT = 16384.0
+CODES = "float8_e4m3fn_x4"
+
+SCRATCH = {
+    "flb": ("sbuf", [128, 16], "int32"),
+    "ft": ("sbuf", [128, 16], "uint16"), "f4": ("sbuf", [128, 64], "uint16"), "fr": ("sbuf", [128, C], "bfloat16"),
+    "ut": ("sbuf", [128, 512], "bfloat16"), "uq": ("sbuf", [128, 128], CODES), "up": ("sbuf", [128, 128], "uint8"),
+    "urq": ("sbuf", [128, 128], CODES), "urp": ("sbuf", [128, 128], "uint8"),
+    "vt": ("sbuf", [128, 512], "bfloat16"), "vq": ("sbuf", [128, 128], CODES), "vp": ("sbuf", [128, 128], "uint8"),
+    "wq": ("sbuf", [128, 512], CODES), "wp": ("sbuf", [128, 512], "uint8"),
+    "et": ("sbuf", [128, 2048], "bfloat16"), "eq": ("sbuf", [128, 512], CODES), "ep": ("sbuf", [128, 512], "uint8"),
+    "xf": ("sbuf", [128, 1024], "bfloat16"), "qf": ("sbuf", [128, C], CODES), "pf": ("sbuf", [128, C], "uint8"),
+    "zt": ("sbuf", [128, 1024], "bfloat16"), "qz": ("sbuf", [128, C], CODES), "pz": ("sbuf", [128, C], "uint8"),
+    "fh": ("sbuf", [128, 1024], "bfloat16"), "zf": ("sbuf", [128, 1024], "bfloat16"), "pb": ("sbuf", [128, 1024], "float32"),
+    "wi": ("sbuf", [128, 512], "bfloat16"), "if32": ("sbuf", [128, 512], "float32"), "col4": ("sbuf", [128, 1], "float32"),
+    "jm": ("sbuf", [128, C], "int32"), "jr": ("sbuf", [128, C], "int32"), "jm2": ("sbuf", [128, C], "int32"), "jr2": ("sbuf", [128, C], "int32"),
+    "thr": ("sbuf", [128, C], "float32"), "rst": ("sbuf", [128, C], "bfloat16"), "cu": ("sbuf", [128, C], "bfloat16"),
+    "k1": ("sbuf", [128, C], "float32"), "k2": ("sbuf", [128, C], "float32"), "sc0": ("sbuf", [128, 1], "float32"), "scc": ("sbuf", [128, 1], "float32"),
+    "pq": ("sbuf", [128, 16], "int32"), "pq2": ("sbuf", [128, 16], "int32"), "cj": ("sbuf", [128, 16], "float32"),
+    "jj": ("sbuf", [128, 16], "float32"), "jh": ("sbuf", [128, 16], "float32"), "oi": ("sbuf", [128, 8], "int32"), "ou": ("sbuf", [128, 8], "uint16"),
+    "mb": ("sbuf", [128, C], "bfloat16"), "ms": ("sbuf", [128, C], "bfloat16"), "scn": ("sbuf", [128, C], "float32"),
+    "eh": ("sbuf", [128, 16], "float32"), "ea": ("sbuf", [128, 16], "float32"), "ed": ("sbuf", [128, 16], "float32"), "en": ("sbuf", [128, 16], "float32"),
+    "t1": ("sbuf", [128, 16], "float32"), "ts": ("sbuf", [128, 32], "float32"), "t0": ("sbuf", [128, 32], "uint16"),
+    "tt": ("sbuf", [128, 128], "uint16"), "wa": ("sbuf", [128, 512], "bfloat16"), "wb": ("sbuf", [128, 512], "bfloat16"),
+    "ar": ("sbuf", [128, C], "bfloat16"), "at": ("sbuf", [128, 16], "uint16"),
+    "ir": ("sbuf", [128, C], "bfloat16"), "it": ("sbuf", [128, 16], "uint16"),
+    "lnf": ("sbuf", [128, C], "float32"), "yb": ("sbuf", [128, C], "float32"),
+    "psa": ("psum", [128, 2048], "float32"), "psb": ("psum", [128, 2048], "float32"),
+    "el0": ("sbuf", [128, 16], "int32"), "el1": ("sbuf", [128, 16], "uint16"), "el2": ("sbuf", [128, 16], "uint16"),
+}
+for _k in range(4):
+    SCRATCH["xt%d" % _k] = ("sbuf", [128, 1024], "bfloat16")
+    SCRATCH["qx%d" % _k] = ("sbuf", [128, C], CODES)
+    SCRATCH["px%d" % _k] = ("sbuf", [128, C], "uint8")
+for _k in range(3):
+    SCRATCH["lq%d" % _k] = ("sbuf", [128, C], CODES)
+    SCRATCH["lp%d" % _k] = ("sbuf", [128, C], "uint8")
+    SCRATCH["st%d" % _k] = ("sbuf", [128, 16], "bfloat16")
+    SCRATCH["sl%d" % _k] = ("sbuf", [128, 16], "bfloat16")
+    SCRATCH["rr%d" % _k] = ("sbuf", [128, C], "bfloat16")
+    SCRATCH["rt%d" % _k] = ("sbuf", [128, 16], "uint16")
+SEMAPHORES = (["cv", "cs", "cp", "cg", "lo", "lf", "lx", "lu", "lv", "lw", "lws", "out"]
+              + ["%s%d" % (a, k) for a in ("ar_s", "ar_l", "ar_d") for k in range(3)])
+
+
+def rank_program(g, core, T, topo):
+    rank = T.rank_of(core)
+    if rank is None:
+        return
+    V, S, P = g.vector, g.scalar, g.tensor
+    queues = {"v": V, "s": S, "p": P, "g": g, "y": g.sync}
+    own = {"v": "cv", "s": "cs", "p": "cp", "g": "cg"}
+    known = {q: {} for q in queues}
+    snap = {}
+    total = {}
+    wrote, read = {}, {}
+
+    def covered(k, d):
+        return k.get(d[0], 0) >= d[1]
+
+    def wait(q, deps):
+        deps = [d for d in dict.fromkeys(deps) if not covered(known[q], d)]
+        best = {}
+        for s, n in deps:
+            best[s] = max(best.get(s, 0), n)
+        deps = list(best.items())
+        for d in deps:
+            if any(o != d and covered(snap[o], d) for o in deps):
+                continue
+            queues[q].wait_ge(T.sem[d[0]], d[1])
+        for d in deps:
+            known[q][d[0]] = max(known[q].get(d[0], 0), d[1])
+            for s, n in snap[d].items():
+                known[q][s] = max(known[q].get(s, 0), n)
+
+    def needs(reads, writes):
+        deps = [wrote[t] for t in reads]
+        for t in writes:
+            if t in wrote:
+                deps.append(wrote[t])
+            deps += read.get(t, [])
+        return deps
+
+    def op(q, call, reads, writes, sem=None, inc=1):
+        wait(q, needs(reads, writes))
+        name = sem or own[q]
+        ins = call()
+        ins.then_inc(T.sem[name], inc)
+        total[name] = total.get(name, 0) + inc
+        me = (name, total[name])
+        snap[me] = dict(known[q])
+        for t in reads:
+            read.setdefault(t, []).append(me)
+        for t in writes:
+            wrote[t], read[t] = me, []
+
+    def arrives(sem, n, tokens):
+        total[sem] = total.get(sem, 0) + n
+        for t in tokens:
+            wrote[t] = (sem, total[sem])
+        snap[(sem, total[sem])] = {}
+
+    def send(dst, out, in_, sem, reads):
+        wait("g", needs(reads, []))
+        rid, pid, _ = topo.addr(dst)
+        g.remote_dma(out, in_, T.sem[sem], T.sem.lo, pid, rid, topo.mask(core, dst))
+        total["lo"] = total.get("lo", 0) + len(topo.engines(core, dst))
+
+    def tcopy(out, in_, r, w):
+        op("v", lambda: V.tensor_copy(out, in_), r, w)
+
+    def tts(out, in0, s1, s2, o0, o1, r, w):
+        if o1 is None:
+            op("v", lambda: V.tensor_scalar(out, in0, s1, None, o0), r, w)
+        else:
+            op("v", lambda: V.tensor_scalar(out, in0, s1, s2, o0, o1), r, w)
+
+    def ttt(out, a, b, o, r, w):
+        op("v", lambda: V.tensor_tensor(out, a, b, o), r, w)
+
+    def quant(q, p, t, r, w):
+        op("v", lambda: V.quantize_mx(q, p, t), r, w)
+
+    def act(out, in_, r, w, scale=None):
+        if scale is None:
+            op("s", lambda: S.activation(out, in_, COPY), r, w)
+        else:
+            op("s", lambda: S.activation(out, in_, COPY, scale=scale), r, w)
+
+    def mm(out, a, ap, b, bp, start, stop, r, w):
+        op("p", lambda: P.matmul_mx(out, a, ap, b, bp, start, stop), r, w)
+
+    def iota(out, pattern, base, cm, w, small=False):
+        if small:
+            op("g", lambda: g.iota(out, pattern, base, cm, allow_small_or_imprecise_dtypes=True), [], w)
+        else:
+            op("g", lambda: g.iota(out, pattern, base, cm), [], w)
+
+    def scan_to(out, row, bias, r, w):
+        op("v", lambda: V.tensor_tensor_scan(T.scn[:, 0:C], T.cu[:, 0:C], row, 0.0, AluOpType.mult, AluOpType.add), r + ["cu"], ["scn"])
+        tts(out, T.scn[:, 15:C:16], T.scc[:, 0:1], bias, AluOpType.mult, AluOpType.add, ["scn", "scc"], w)
+
+    A = AluOpType
+    op("s", lambda: S.dma_start(T.flb[:], T.fl[:]), [], ["flb"], "lf", 16)
+    op("y", lambda: g.sync.dma_start(T.xt0[:], T.x[:]), [], ["xt0.%d" % b for b in range(4)], "lx", 16)
+    op("s", lambda: S.dma_start(T.ut[:], T.u[:]), [], ["ut"], "lu", 16)
+    op("s", lambda: S.dma_start(T.wq[:, 0:512].bitcast(dt.uint8), T.wc[:]), [], ["wq"], "lw", 16)
+    op("y", lambda: g.sync.dma_start(T.wp[:, 0:512], T.ws[:]), [], ["wp"], "lws", 16)
+    op("y", lambda: g.sync.dma_start(T.vt[:], T.v[:]), [], ["vt"], "lv", 16)
+    iota(T.jm[:], [[1, C]], 0, -1, ["jm"])
+    iota(T.oi[:], [[16, 8]], 0, 0, ["oi"])
+    iota(T.jr[:], [[1, C]], 0, 0, ["jr"])
+    iota(T.pq[:], [[0, 16]], 0, 1, ["pq"])
+    iota(T.cj[:], [[16, 16]], 256, 0, ["cj"], True)
+    first = T.cores[rank ^ ROUNDS[0]]
+    send(first, T.el0[:], T.flb[:], "ar_l0", ["flb"])
+    arrives("ar_l0", len(topo.engines(first, core)), ["el0"])
+    iota(T.wi[:], [[1, 512]], -256, 0, ["wi"], True)
+    iota(T.if32[:], [[1, 512]], 0, 0, ["if32"], True)
+    iota(T.col4[:], [[0, 1]], 0, 4, ["col4"], True)
+    tcopy(T.ou[:], T.oi[:], ["oi"], ["ou"])
+    tts(T.jm2[:], T.jm[:], 15, None, A.bitwise_and, None, ["jm"], ["jm2"])
+    tts(T.thr[:], T.jm2[:], 0.0, 1.0e29, A.not_equal, A.mult, ["jm2"], ["thr"])
+    tts(T.jr2[:], T.jr[:], 15, None, A.bitwise_and, None, ["jr"], ["jr2"])
+    tts(T.rst[:], T.jr2[:], 0.0, None, A.not_equal, None, ["jr2"], ["rst"])
+    quant(T.uq[:, 0:128], T.up[:, 0:128], T.ut[:, 0:512], ["ut"], ["uq"])
+    op("v", lambda: V.tensor_copy(T.urq[:, 0:128].bitcast(dt.uint32), T.uq[:, 0:128].bitcast(dt.uint32).indirect(T.ou[:, 0:8])), ["uq", "ou"], ["urq"])
+    tcopy(T.urp[:, 0:128], T.up[:, 0:128].indirect(T.ou[:, 0:8]), ["uq", "ou"], ["urp"])
+
+    def late_constants():
+        for b in range(4):
+            tts(T.et[:, 512 * b:512 * b + 512], T.if32[:], float(b), T.col4[:, 0:1], A.subtract, A.is_equal, ["if32", "col4"], ["et%d" % b])
+        quant(T.eq[:, 0:512], T.ep[:, 0:512], T.et[:, 0:2048], ["et%d" % b for b in range(4)], ["eq"])
+        tcopy(T.ft[:], T.flb[:], ["flb"], ["ft"])
+
+    def later_constants():
+        tts(T.pq2[:], T.pq[:], 15, None, A.bitwise_and, None, ["pq"], ["pq2"])
+        tts(T.k1[:], T.jm2[:], 1.0, LIFT - 1.0, A.is_equal, A.mult, ["jm2"], ["k1"])
+        tts(T.k2[:], T.jm2[:], 0.0, None, A.not_equal, None, ["jm2"], ["k2"])
+        tts(T.sc0[:], T.jm2[:, 15:16], 0.0, 1.0 - 1.0 / LIFT, A.is_equal, A.mult, ["jm2"], ["sc0"])
+        ttt(T.jj[:], T.pq2[:], T.cj[:], A.add, ["pq2", "cj"], ["jj"])
+        ttt(T.cu[:], T.k1[:], T.k2[:], A.add, ["k1", "k2"], ["cu"])
+        tts(T.jh[:], T.jj[:], 0.5, None, A.mult, None, ["jj"], ["jh"])
+        tts(T.scc[:], T.sc0[:], 1.0 / LIFT, None, A.add, None, ["sc0"], ["scc"])
+        act(T.wa[:, C:2 * C], T.wi[:, C:2 * C], ["wi"], ["wa.k"])
+        act(T.wb[:, C:2 * C], T.wi[:, C:2 * C], ["wi"], ["wb.k"])
+
+    win = (T.wa, T.wb)
+    wn = ("wa", "wb")
+    for k, m in enumerate(ROUNDS):
+        d = T.cores[rank ^ m]
+        ne = len(topo.engines(d, core))
+        xt, qx, px = T["xt%d" % k], T["qx%d" % k], T["px%d" % k]
+        lq, lp, st, sl, el = T["lq%d" % k], T["lp%d" % k], T["st%d" % k], T["sl%d" % k], T["el%d" % k]
+        rr, rt = T["rr%d" % k], T["rt%d" % k]
+        Xt = ["xt%d.%d" % (k, b) for b in range(4)]
+        quant(qx[:, 0:C], px[:, 0:C], xt[:, 0:1024], Xt, ["qx%d" % k])
+        mm(T.psb[:, 0:C], T.urq[:, 0:128], T.urp[:, 0:128], qx[:, 0:C], px[:, 0:C], True, True, ["urq", "urp", "qx%d" % k], ["psb0"])
+        ttt(T.mb[:], T.psb[:, 0:C], T.thr[:], A.is_gt, ["psb0", "thr"], ["mb"])
+        op("v", lambda: V.tensor_tensor_scan(T.ms[:], T.rst[:], T.mb[:], 0.0, A.mult, A.add), ["rst", "mb"], ["ms"])
+        tts(st[:], T.ms[:, 15:C:16], 2.0, -1.0, A.mult, A.add, ["ms"], ["st%d" % k])
+        send(d, sl[:], st[:], "ar_s%d" % k, ["st%d" % k])
+        arrives("ar_s%d" % k, ne, ["sl%d" % k])
+        send(d, lq[:, 0:C].bitcast(dt.uint8), qx[:, 0:C].bitcast(dt.uint8), "ar_d%d" % k, ["qx%d" % k])
+        send(d, lp[:, 0:C], px[:, 0:C], "ar_d%d" % k, ["qx%d" % k])
+        arrives("ar_d%d" % k, 2 * ne, ["lq%d" % k])
+        if k == 0:
+            late_constants()
+        fsrc, fname = (T.ft, "ft") if k == 0 else (T["rt%d" % (k - 1)], "rt%d" % (k - 1))
+        frow, frname = (T.fr, "fr") if k == 0 else (T["rr%d" % (k - 1)], "rr%d" % (k - 1))
+        for b in (2, 3, 0, 1):
+            tts(T.f4[:, 16 * b:16 * b + 16], fsrc[:], 4.0, float(b), A.mult, A.add, [fname], ["f4.%d" % b])
+        for b in (2, 3):
+            act(T.xf[:, b:1024:4], xt[:, 0:1024].indirect(T.f4[:, 16 * b:16 * b + 16]), Xt + ["f4.%d" % b], ["xf%d" % b])
+        for b in (0, 1):
+            tcopy(T.xf[:, b:1024:4], xt[:, 0:1024].indirect(T.f4[:, 16 * b:16 * b + 16]), Xt + ["f4.%d" % b], ["xf%d" % b])
+        if k == 0:
+            later_constants()
+            act(T.fr[:], T.wi[:, C:2 * C].indirect(T.ft[:, 0:16]), ["wi", "ft"], ["fr"])
+        tts(T.eh[:], el[:], 0.5, None, A.mult, None, ["el%d" % k], ["eh"])
+        ttt(T.ed[:], T.eh[:], T.jh[:], A.subtract, ["eh", "jh"], ["ed"])
+        ttt(T.ea[:], T.eh[:], T.jh[:], A.add, ["eh", "jh"], ["ea"])
+        ttt(T.en[:], T.ed[:], st[:], A.mult, ["ed", "st%d" % k], ["en"])
+        quant(T.qf[:, 0:C], T.pf[:, 0:C], T.xf[:, 0:1024], ["xf%d" % b for b in range(4)], ["qf"])
+        if k == 0:
+            quant(T.vq[:, 0:128], T.vp[:, 0:128], T.vt[:, 0:512], ["vt"], ["vq"])
+        for b in range(4):
+            mm(T.psa[:, 512 * b:512 * b + C], T.eq[:, 128 * b:128 * b + 128], T.ep[:, 128 * b:128 * b + 128], qx[:, 0:C], px[:, 0:C], True, True,
+               ["eq", "qx%d" % k], ["psa%d" % b])
+        for b in range(4):
+            act(T.fh[:, C * b:C * b + C], T.psa[:, 512 * b:512 * b + C], ["psa%d" % b], ["fh%d" % b], 0.5)
+        for b in range(4):
+            e, ep, o = T.eq[:, 128 * b:128 * b + 128], T.ep[:, 128 * b:128 * b + 128], T.psb[:, 512 * b:512 * b + C]
+            mm(o, e, ep, T.qf[:, 0:C], T.pf[:, 0:C], True, False, ["eq", "qf"], ["psb%d" % b])
+            mm(o, e, ep, lq[:, 0:C], lp[:, 0:C], False, True, ["eq", "lq%d" % k], ["psb%d" % b])
+
+        def meet(b):
+            act(T.zf[:, C * b:C * b + C], T.psb[:, 512 * b:512 * b + C], ["psb%d" % b], ["zf%d" % b], 0.5)
+
+        def hop(out, w, window, reads, off, oname, c0):
+            tcopy(out[:, 0:128], window.indirect(off[:, c0:c0 + 8]), reads + [oname], [w + ".v"])
+            act(out[:, 128:C], window.indirect(off[:, c0 + 8:c0 + 16]), reads + [oname], [w + ".s"])
+
+        ttt(T.t1[:], sl[:], T.en[:], A.mult, ["sl%d" % k, "en"], ["t1"])
+        ttt(T.ts[:, 0:16], T.t1[:], T.ea[:], A.add, ["t1", "ea"], ["ts0"])
+        ttt(T.ts[:, 16:32], T.ea[:], T.t1[:], A.subtract, ["t1", "ea"], ["ts1"])
+        tcopy(T.t0[:], T.ts[:], ["ts0", "ts1"], ["t0"])
+        hop(T.wa, "wa", T.wi[:, 0:512], ["wi"], T.t0, "t0", 0)
+        off, oname, c0 = T.t0, "t0", 0
+        for i in range(8):
+            a, b = i % 2, 1 - i % 2
+            hop(win[b], wn[b], win[a][:, 0:512], [wn[a] + ".v", wn[a] + ".s", wn[a] + ".k"], off, oname, c0)
+            if i < 7:
+                if i >= 4:
+                    meet(i - 4)
+                scan_to(T.tt[:, 16 * i:16 * i + 16], win[b][:, 0:C], 256.25, [wn[b] + ".v", wn[b] + ".s"], ["tt%d" % i])
+                off, oname, c0 = T.tt, "tt%d" % i, 16 * i
+        hop(T.ar, "ar", T.wa[:, 0:512], ["wa.v", "wa.s", "wa.k"], T.t0, "t0", 16)
+        meet(3)
+        scan_to(T.at[:], T.ar[:], 0.25, ["ar.v", "ar.s"], ["at"])
+        act(rr[:], frow[:, 0:C].indirect(T.at[:, 0:16]), [frname, "at"], ["rr%d" % k])
+        for b in range(4):
+            f = tcopy if b == 0 else act
+            f(T.zt[:, b:1024:4], T.zf[:, C * b:C * b + C].indirect(T.at[:, 0:16]), ["zf%d" % b, "at"], ["zt%d" % b])
+        scan_to(rt[:], rr[:], 0.25, ["rr%d" % k], ["rt%d" % k])
+        if k < 2:
+            nd = T.cores[rank ^ ROUNDS[k + 1]]
+            send(nd, T["el%d" % (k + 1)][:], rt[:], "ar_l%d" % (k + 1), ["rt%d" % k])
+            arrives("ar_l%d" % (k + 1), len(topo.engines(nd, core)), ["el%d" % (k + 1)])
+        tcopy(T.ir[:, 0:C].indirect(rt[:, 0:16]), T.wi[:, C:2 * C], ["wi", "rt%d" % k], ["ir"])
+        quant(T.qz[:, 0:C], T.pz[:, 0:C], T.zt[:, 0:1024], ["zt%d" % b for b in range(4)], ["qz"])
+        scan_to(T.it[:], T.ir[:], 0.25, ["ir"], ["it"])
+        for b in range(4):
+            mm(T.psb[:, 512 * b:512 * b + C], T.wq[:, 128 * b:128 * b + 128], T.wp[:, 128 * b:128 * b + 128], T.qz[:, 0:C], T.pz[:, 0:C], True, True,
+               ["wq", "wp", "qz"], ["psb%d" % b])
+        xn = T["xt%d" % (k + 1)]
+        for b in range(4):
+            act(T.pb[:, C * b:C * b + C], T.psb[:, 512 * b:512 * b + C], ["psb%d" % b], ["pb%d" % b], 0.015625)
+            ttt(xn[:, b:1024:4], T.pb[:, C * b:C * b + C].indirect(T.it[:, 0:16]), T.fh[:, C * b:C * b + C], A.add,
+                ["pb%d" % b, "it", "fh%d" % b], ["xt%d.%d" % (k + 1, b)])
+    act(T.lnf[:], T.rr2[:], ["rr2"], ["lnf"])
+    op("y", lambda: g.sync.dma_start(T.ln[:], T.lnf[0:128:16, :]), ["lnf"], ["ln"], "out", 16)
+    quant(T.qx3[:, 0:C], T.px3[:, 0:C], T.xt3[:, 0:1024], ["xt3.%d" % b for b in range(4)], ["qx3"])
+    for h in range(2):
+        mm(T.psa[:, 512 * h:512 * h + 128], T.vq[:, 0:128], T.vp[:, 0:128], T.qx3[:, 128 * h:128 * h + 128], T.px3[:, 128 * h:128 * h + 128], True, True,
+           ["vq", "qx3"], ["psa%d" % h])
+    op("y", lambda: g.sync.dma_start(T.oc[:, 0:4 * C], T.qx3[:, 0:C].bitcast(dt.uint8)), ["qx3"], ["oc"], "out", 16)
+
+    def scales(q, queue, i):
+        op(q, lambda: queue.dma_start(T.osc[4 * i:4 * i + 4, 0:C], T.px3[32 * i:32 * i + 4, 0:C]), ["qx3"], ["osc%d" % i], "out", 16)
+
+    scales("y", g.sync, 0)
+    scales("y", g.sync, 1)
+    tcopy(T.yb[:, 0:128], T.psa[:, 0:128], ["psa0"], ["y0"])
+    act(T.yb[:, 128:C], T.psa[:, 512:640], ["psa1"], ["y1"])
+    op("y", lambda: g.sync.dma_start(T.y[:, 0:128], T.yb[:, 0:128]), ["y0"], ["yo0"], "out", 16)
+    op("s", lambda: S.dma_start(T.y[:, 128:C], T.yb[:, 128:C]), ["y1"], ["yo1"], "out", 16)
+    scales("s", S, 2)
+    scales("s", S, 3)
+    for s, n in sorted(total.items()):
+        g.wait_ge(T.sem[s], n)

@@ -1,9 +1,9 @@
-from concourse.bass import IndirectOffsetOnAxis
 from concourse.mybir import dt, AluOpType, ActivationFunctionType
 
 C = 256
 ROUNDS = (1, 2, 4)
 COPY = ActivationFunctionType.Copy
+IDENTITY = ActivationFunctionType.Identity
 LIFT = 16384.0
 CODES = "float8_e4m3fn_x4"
 
@@ -14,22 +14,22 @@ SCRATCH = {
     "urq": ("sbuf", [128, 128], CODES), "urp": ("sbuf", [128, 128], "uint8"),
     "vt": ("sbuf", [128, 512], "bfloat16"), "vq": ("sbuf", [128, 128], CODES), "vp": ("sbuf", [128, 128], "uint8"),
     "wq": ("sbuf", [128, 512], CODES), "wp": ("sbuf", [128, 512], "uint8"),
-    "et": ("sbuf", [128, 2048], "bfloat16"), "eq": ("sbuf", [128, 512], CODES), "ep": ("sbuf", [128, 512], "uint8"),
+    "ew": ("sbuf", [128, 516], "bfloat16"), "eq": ("sbuf", [128, 512], CODES), "ep": ("sbuf", [128, 512], "uint8"),
     "xf": ("sbuf", [128, 1024], "bfloat16"), "qf": ("sbuf", [128, C], CODES), "pf": ("sbuf", [128, C], "uint8"),
     "zt": ("sbuf", [128, 1024], "bfloat16"), "qz": ("sbuf", [128, C], CODES), "pz": ("sbuf", [128, C], "uint8"),
     "fh": ("sbuf", [128, 1024], "bfloat16"), "zf": ("sbuf", [128, 1024], "bfloat16"), "pb": ("sbuf", [128, 1024], "float32"),
-    "wi": ("sbuf", [128, 512], "bfloat16"), "if32": ("sbuf", [128, 512], "float32"), "col4": ("sbuf", [128, 1], "float32"),
-    "jm": ("sbuf", [128, C], "int32"), "jr": ("sbuf", [128, C], "int32"), "jm2": ("sbuf", [128, C], "int32"), "jr2": ("sbuf", [128, C], "int32"),
+    "wi": ("sbuf", [128, 512], "bfloat16"), "ie": ("sbuf", [128, 516], "float32"), "ia": ("sbuf", [128, 516], "float32"),
+    "wcol": ("sbuf", [128, 1], "float32"), "jm": ("sbuf", [128, C], "int32"), "jm2": ("sbuf", [128, C], "int32"),
     "thr": ("sbuf", [128, C], "float32"), "rst": ("sbuf", [128, C], "bfloat16"), "cu": ("sbuf", [128, C], "bfloat16"),
-    "k1": ("sbuf", [128, C], "float32"), "k2": ("sbuf", [128, C], "float32"), "sc0": ("sbuf", [128, 1], "float32"), "scc": ("sbuf", [128, 1], "float32"),
+    "k1": ("sbuf", [128, C], "float32"), "sc0": ("sbuf", [128, 1], "float32"), "scc": ("sbuf", [128, 1], "float32"),
     "pq": ("sbuf", [128, 16], "int32"), "pq2": ("sbuf", [128, 16], "int32"), "cj": ("sbuf", [128, 16], "float32"),
     "jj": ("sbuf", [128, 16], "float32"), "jh": ("sbuf", [128, 16], "float32"), "oi": ("sbuf", [128, 8], "int32"), "ou": ("sbuf", [128, 8], "uint16"),
-    "mb": ("sbuf", [128, C], "bfloat16"), "ms": ("sbuf", [128, C], "bfloat16"), "scn": ("sbuf", [128, C], "float32"),
-    "eh": ("sbuf", [128, 16], "float32"), "ea": ("sbuf", [128, 16], "float32"), "ed": ("sbuf", [128, 16], "float32"), "en": ("sbuf", [128, 16], "float32"),
-    "t1": ("sbuf", [128, 16], "float32"), "ts": ("sbuf", [128, 32], "float32"), "t0": ("sbuf", [128, 32], "uint16"),
-    "tt": ("sbuf", [128, 128], "uint16"), "wa": ("sbuf", [128, 512], "bfloat16"), "wb": ("sbuf", [128, 512], "bfloat16"),
+    "mb": ("sbuf", [128, C], "bfloat16"), "ms": ("sbuf", [128, C], "bfloat16"), "scn": ("sbuf", [128, C], "float32"), "scr": ("sbuf", [128, C], "float32"),
+    "eh": ("sbuf", [128, 16], "float32"), "ed": ("sbuf", [128, 16], "float32"),
+    "pk": ("sbuf", [128, 48], "float32"), "ts": ("sbuf", [128, 48], "float32"), "t0": ("sbuf", [128, 32], "uint16"),
+    "tt": ("sbuf", [128, 48], "uint16"), "wa": ("sbuf", [128, 512], "bfloat16"), "wb": ("sbuf", [128, 512], "bfloat16"),
     "ar": ("sbuf", [128, C], "bfloat16"), "at": ("sbuf", [128, 16], "uint16"),
-    "ir": ("sbuf", [128, C], "bfloat16"), "it": ("sbuf", [128, 16], "uint16"),
+    "ir": ("sbuf", [128, C], "bfloat16"), "iv": ("sbuf", [128, C], "bfloat16"),
     "lnf": ("sbuf", [128, C], "float32"), "yb": ("sbuf", [128, C], "float32"),
     "psa": ("psum", [128, 2048], "float32"), "psb": ("psum", [128, 2048], "float32"),
     "el0": ("sbuf", [128, 16], "int32"), "el1": ("sbuf", [128, 16], "uint16"), "el2": ("sbuf", [128, 16], "uint16"),
@@ -41,10 +41,11 @@ for _k in range(4):
 for _k in range(3):
     SCRATCH["lq%d" % _k] = ("sbuf", [128, C], CODES)
     SCRATCH["lp%d" % _k] = ("sbuf", [128, C], "uint8")
-    SCRATCH["st%d" % _k] = ("sbuf", [128, 16], "bfloat16")
-    SCRATCH["sl%d" % _k] = ("sbuf", [128, 16], "bfloat16")
+    SCRATCH["st%d" % _k] = ("sbuf", [128, 48], "bfloat16")
+    SCRATCH["sl%d" % _k] = ("sbuf", [128, 48], "bfloat16")
     SCRATCH["rr%d" % _k] = ("sbuf", [128, C], "bfloat16")
     SCRATCH["rt%d" % _k] = ("sbuf", [128, 16], "uint16")
+    SCRATCH["it%d" % _k] = ("sbuf", [128, 16], "uint16")
 SEMAPHORES = (["cv", "cs", "cp", "cg", "lo", "lf", "lx", "lu", "lv", "lw", "lws", "out"]
               + ["%s%d" % (a, k) for a in ("ar_s", "ar_l", "ar_d") for k in range(3)])
 
@@ -65,10 +66,10 @@ def rank_program(g, core, T, topo):
         return k.get(d[0], 0) >= d[1]
 
     def wait(q, deps):
-        deps = [d for d in dict.fromkeys(deps) if not covered(known[q], d)]
         best = {}
-        for s, n in deps:
-            best[s] = max(best.get(s, 0), n)
+        for d in deps:
+            if not covered(known[q], d):
+                best[d[0]] = max(best.get(d[0], 0), d[1])
         deps = list(best.items())
         for d in deps:
             if any(o != d and covered(snap[o], d) for o in deps):
@@ -124,6 +125,9 @@ def rank_program(g, core, T, topo):
     def ttt(out, a, b, o, r, w):
         op("v", lambda: V.tensor_tensor(out, a, b, o), r, w)
 
+    def fill(ap, value, w):
+        op("v", lambda: V.memset(ap, value), [], w)
+
     def quant(q, p, t, r, w):
         op("v", lambda: V.quantize_mx(q, p, t), r, w)
 
@@ -142,54 +146,60 @@ def rank_program(g, core, T, topo):
         else:
             op("g", lambda: g.iota(out, pattern, base, cm), [], w)
 
-    def scan_to(out, row, bias, r, w):
-        op("v", lambda: V.tensor_tensor_scan(T.scn[:, 0:C], T.cu[:, 0:C], row, 0.0, AluOpType.mult, AluOpType.add), r + ["cu"], ["scn"])
-        tts(out, T.scn[:, 15:C:16], T.scc[:, 0:1], bias, AluOpType.mult, AluOpType.add, ["scn", "scc"], w)
-
     A = AluOpType
+
+    def scan(row, r, w="scn"):
+        op("v", lambda: V.tensor_tensor_scan(T[w][:, 0:C], T.cu[:, 0:C], row, 0.0, A.mult, A.add), r + ["cu"], [w])
+
+    def table(out, bias, w, s="scn"):
+        tts(out, T[s][:, 15:C:16], T.scc[:, 0:1], bias, A.mult, A.add, [s, "scc"], w)
+
+    spare = []
+
+    def hop(out, w, window, reads, off, oname, c0):
+        tcopy(out[:, 0:128], window.indirect(off[:, c0:c0 + 8]), reads + [oname], [w + ".v"])
+        act(out[:, 128:C], window.indirect(off[:, c0 + 8:c0 + 16]), reads + [oname], [w + ".s"])
+        if spare:
+            spare.pop(0)()
+
     op("s", lambda: S.dma_start(T.flb[:], T.fl[:]), [], ["flb"], "lf", 16)
     op("y", lambda: g.sync.dma_start(T.xt0[:], T.x[:]), [], ["xt0.%d" % b for b in range(4)], "lx", 16)
     op("s", lambda: S.dma_start(T.ut[:], T.u[:]), [], ["ut"], "lu", 16)
-    op("s", lambda: S.dma_start(T.wq[:, 0:512].bitcast(dt.uint8), T.wc[:]), [], ["wq"], "lw", 16)
+    wait("y", [wrote["xt0.0"]])
+    op("y", lambda: g.sync.dma_start(T.wq[:, 0:512].bitcast(dt.uint8), T.wc[:]), [], ["wq"], "lw", 16)
     op("y", lambda: g.sync.dma_start(T.wp[:, 0:512], T.ws[:]), [], ["wp"], "lws", 16)
     op("y", lambda: g.sync.dma_start(T.vt[:], T.v[:]), [], ["vt"], "lv", 16)
     iota(T.jm[:], [[1, C]], 0, -1, ["jm"])
     iota(T.oi[:], [[16, 8]], 0, 0, ["oi"])
-    iota(T.jr[:], [[1, C]], 0, 0, ["jr"])
     iota(T.pq[:], [[0, 16]], 0, 1, ["pq"])
     iota(T.cj[:], [[16, 16]], 256, 0, ["cj"], True)
+    iota(T.wcol[:], [[0, 1]], -252, 4, ["wcol"], True)
+    iota(T.ie[:], [[1, 516]], -4, -4, ["ie"], True)
     first = T.cores[rank ^ ROUNDS[0]]
     send(first, T.el0[:], T.flb[:], "ar_l0", ["flb"])
     arrives("ar_l0", len(topo.engines(first, core)), ["el0"])
-    iota(T.wi[:], [[1, 512]], -256, 0, ["wi"], True)
-    iota(T.if32[:], [[1, 512]], 0, 0, ["if32"], True)
-    iota(T.col4[:], [[0, 1]], 0, 4, ["col4"], True)
-    tcopy(T.ou[:], T.oi[:], ["oi"], ["ou"])
+    fill(T.st0[:], -1.0, ["st0"])
+    fill(T.st0[:, 0:48:3], 0.0, ["st0"])
     tts(T.jm2[:], T.jm[:], 15, None, A.bitwise_and, None, ["jm"], ["jm2"])
+    tcopy(T.ou[:], T.oi[:], ["oi"], ["ou"])
     tts(T.thr[:], T.jm2[:], 0.0, 1.0e29, A.not_equal, A.mult, ["jm2"], ["thr"])
-    tts(T.jr2[:], T.jr[:], 15, None, A.bitwise_and, None, ["jr"], ["jr2"])
-    tts(T.rst[:], T.jr2[:], 0.0, None, A.not_equal, None, ["jr2"], ["rst"])
+    tts(T.rst[:], T.jm2[:], 0.0, None, A.not_equal, None, ["jm2"], ["rst"])
+    tts(T.k1[:], T.jm2[:], 1.0, LIFT - 1.0, A.is_equal, A.mult, ["jm2"], ["k1"])
+    tts(T.sc0[:], T.jm2[:, 15:16], 0.0, 1.0 - 1.0 / LIFT, A.is_equal, A.mult, ["jm2"], ["sc0"])
+    tts(T.pq2[:], T.pq[:], 15, None, A.bitwise_and, None, ["pq"], ["pq2"])
+    ttt(T.cu[:], T.k1[:], T.rst[:], A.add, ["k1", "rst"], ["cu"])
+    tts(T.scc[:], T.sc0[:], 1.0 / LIFT, None, A.add, None, ["sc0"], ["scc"])
+    ttt(T.jj[:], T.pq2[:], T.cj[:], A.add, ["pq2", "cj"], ["jj"])
     quant(T.uq[:, 0:128], T.up[:, 0:128], T.ut[:, 0:512], ["ut"], ["uq"])
+    tts(T.jh[:], T.jj[:], 0.5, None, A.mult, None, ["jj"], ["jh"])
     op("v", lambda: V.tensor_copy(T.urq[:, 0:128].bitcast(dt.uint32), T.uq[:, 0:128].bitcast(dt.uint32).indirect(T.ou[:, 0:8])), ["uq", "ou"], ["urq"])
     tcopy(T.urp[:, 0:128], T.up[:, 0:128].indirect(T.ou[:, 0:8]), ["uq", "ou"], ["urp"])
-
-    def late_constants():
-        for b in range(4):
-            tts(T.et[:, 512 * b:512 * b + 512], T.if32[:], float(b), T.col4[:, 0:1], A.subtract, A.is_equal, ["if32", "col4"], ["et%d" % b])
-        quant(T.eq[:, 0:512], T.ep[:, 0:512], T.et[:, 0:2048], ["et%d" % b for b in range(4)], ["eq"])
-        tcopy(T.ft[:], T.flb[:], ["flb"], ["ft"])
-
-    def later_constants():
-        tts(T.pq2[:], T.pq[:], 15, None, A.bitwise_and, None, ["pq"], ["pq2"])
-        tts(T.k1[:], T.jm2[:], 1.0, LIFT - 1.0, A.is_equal, A.mult, ["jm2"], ["k1"])
-        tts(T.k2[:], T.jm2[:], 0.0, None, A.not_equal, None, ["jm2"], ["k2"])
-        tts(T.sc0[:], T.jm2[:, 15:16], 0.0, 1.0 - 1.0 / LIFT, A.is_equal, A.mult, ["jm2"], ["sc0"])
-        ttt(T.jj[:], T.pq2[:], T.cj[:], A.add, ["pq2", "cj"], ["jj"])
-        ttt(T.cu[:], T.k1[:], T.k2[:], A.add, ["k1", "k2"], ["cu"])
-        tts(T.jh[:], T.jj[:], 0.5, None, A.mult, None, ["jj"], ["jh"])
-        tts(T.scc[:], T.sc0[:], 1.0 / LIFT, None, A.add, None, ["sc0"], ["scc"])
-        act(T.wa[:, C:2 * C], T.wi[:, C:2 * C], ["wi"], ["wa.k"])
-        act(T.wb[:, C:2 * C], T.wi[:, C:2 * C], ["wi"], ["wb.k"])
+    tcopy(T.ft[:], T.flb[:], ["flb"], ["ft"])
+    op("s", lambda: S.activation(T.ia[:], T.ie[:], ActivationFunctionType.Abs), ["ie"], ["ia"])
+    op("s", lambda: S.activation(T.ew[:], T.ia[:], ActivationFunctionType.Relu, bias=1.0, scale=-1.0), ["ia"], ["ew"])
+    op("s", lambda: S.activation(T.wi[:], T.ie[:, 0:512], IDENTITY, bias=T.wcol[:, 0:1]), ["ie", "wcol"], ["wi"])
+    act(T.wa[:, C:2 * C], T.wi[:, C:2 * C], ["wi"], ["wa.k"])
+    act(T.wb[:, C:2 * C], T.wi[:, C:2 * C], ["wi"], ["wb.k"])
 
     win = (T.wa, T.wb)
     wn = ("wa", "wb")
@@ -198,92 +208,116 @@ def rank_program(g, core, T, topo):
         ne = len(topo.engines(d, core))
         xt, qx, px = T["xt%d" % k], T["qx%d" % k], T["px%d" % k]
         lq, lp, st, sl, el = T["lq%d" % k], T["lp%d" % k], T["st%d" % k], T["sl%d" % k], T["el%d" % k]
-        rr, rt = T["rr%d" % k], T["rt%d" % k]
+        rr, rt, it = T["rr%d" % k], T["rt%d" % k], T["it%d" % k]
         Xt = ["xt%d.%d" % (k, b) for b in range(4)]
         quant(qx[:, 0:C], px[:, 0:C], xt[:, 0:1024], Xt, ["qx%d" % k])
-        mm(T.psb[:, 0:C], T.urq[:, 0:128], T.urp[:, 0:128], qx[:, 0:C], px[:, 0:C], True, True, ["urq", "urp", "qx%d" % k], ["psb0"])
-        ttt(T.mb[:], T.psb[:, 0:C], T.thr[:], A.is_gt, ["psb0", "thr"], ["mb"])
-        op("v", lambda: V.tensor_tensor_scan(T.ms[:], T.rst[:], T.mb[:], 0.0, A.mult, A.add), ["rst", "mb"], ["ms"])
-        tts(st[:], T.ms[:, 15:C:16], 2.0, -1.0, A.mult, A.add, ["ms"], ["st%d" % k])
+        for h in range(2):
+            mm(T.psb[:, 512 * h:512 * h + 128], T.urq[:, 0:128], T.urp[:, 0:128], qx[:, 128 * h:128 * h + 128], px[:, 128 * h:128 * h + 128], True, True,
+               ["urq", "urp", "qx%d" % k], ["psb%d" % h])
+        for h in range(2):
+            ttt(T.mb[:, 128 * h:128 * h + 128], T.psb[:, 512 * h:512 * h + 128], T.thr[:, 128 * h:128 * h + 128], A.is_gt, ["psb%d" % h, "thr"], ["mb%d" % h])
+        op("v", lambda: V.tensor_tensor_scan(T.ms[:], T.rst[:], T.mb[:], 0.0, A.mult, A.add), ["rst", "mb0", "mb1"], ["ms"])
+        tts(st[:, 1:48:3], T.ms[:, 15:C:16], 2.0, -1.0, A.mult, A.add, ["ms"], ["st%d" % k])
         send(d, sl[:], st[:], "ar_s%d" % k, ["st%d" % k])
         arrives("ar_s%d" % k, ne, ["sl%d" % k])
         send(d, lq[:, 0:C].bitcast(dt.uint8), qx[:, 0:C].bitcast(dt.uint8), "ar_d%d" % k, ["qx%d" % k])
         send(d, lp[:, 0:C], px[:, 0:C], "ar_d%d" % k, ["qx%d" % k])
         arrives("ar_d%d" % k, 2 * ne, ["lq%d" % k])
-        if k == 0:
-            late_constants()
         fsrc, fname = (T.ft, "ft") if k == 0 else (T["rt%d" % (k - 1)], "rt%d" % (k - 1))
         frow, frname = (T.fr, "fr") if k == 0 else (T["rr%d" % (k - 1)], "rr%d" % (k - 1))
-        for b in (2, 3, 0, 1):
+        lay = ((1, 2, 3), (0,)) if k == 0 else ((2, 3), (0, 1))
+        for b in lay[0] + lay[1]:
             tts(T.f4[:, 16 * b:16 * b + 16], fsrc[:], 4.0, float(b), A.mult, A.add, [fname], ["f4.%d" % b])
-        for b in (2, 3):
+        for b in lay[0]:
             act(T.xf[:, b:1024:4], xt[:, 0:1024].indirect(T.f4[:, 16 * b:16 * b + 16]), Xt + ["f4.%d" % b], ["xf%d" % b])
-        for b in (0, 1):
+        for b in lay[1]:
             tcopy(T.xf[:, b:1024:4], xt[:, 0:1024].indirect(T.f4[:, 16 * b:16 * b + 16]), Xt + ["f4.%d" % b], ["xf%d" % b])
         if k == 0:
-            later_constants()
+            for b in range(4):
+                quant(T.eq[:, 128 * b:128 * b + 128], T.ep[:, 128 * b:128 * b + 128], T.ew[:, 4 - b:516 - b], ["ew"], ["eq%d" % b])
             act(T.fr[:], T.wi[:, C:2 * C].indirect(T.ft[:, 0:16]), ["wi", "ft"], ["fr"])
         tts(T.eh[:], el[:], 0.5, None, A.mult, None, ["el%d" % k], ["eh"])
         ttt(T.ed[:], T.eh[:], T.jh[:], A.subtract, ["eh", "jh"], ["ed"])
-        ttt(T.ea[:], T.eh[:], T.jh[:], A.add, ["eh", "jh"], ["ea"])
-        ttt(T.en[:], T.ed[:], st[:], A.mult, ["ed", "st%d" % k], ["en"])
+        ttt(T.pk[:, 1:48:3], T.eh[:], T.jh[:], A.add, ["eh", "jh"], ["pk1"])
+        ttt(T.pk[:, 0:48:3], T.ed[:], st[:, 1:48:3], A.mult, ["ed", "st%d" % k], ["pk0"])
+        tts(T.pk[:, 2:48:3], T.pk[:, 1:48:3], 2.0, None, A.mult, None, ["pk1"], ["pk2"])
         quant(T.qf[:, 0:C], T.pf[:, 0:C], T.xf[:, 0:1024], ["xf%d" % b for b in range(4)], ["qf"])
-        if k == 0:
-            quant(T.vq[:, 0:128], T.vp[:, 0:128], T.vt[:, 0:512], ["vt"], ["vq"])
         for b in range(4):
             mm(T.psa[:, 512 * b:512 * b + C], T.eq[:, 128 * b:128 * b + 128], T.ep[:, 128 * b:128 * b + 128], qx[:, 0:C], px[:, 0:C], True, True,
-               ["eq", "qx%d" % k], ["psa%d" % b])
+               ["eq%d" % b, "qx%d" % k], ["psa%d" % b])
         for b in range(4):
             act(T.fh[:, C * b:C * b + C], T.psa[:, 512 * b:512 * b + C], ["psa%d" % b], ["fh%d" % b], 0.5)
         for b in range(4):
             e, ep, o = T.eq[:, 128 * b:128 * b + 128], T.ep[:, 128 * b:128 * b + 128], T.psb[:, 512 * b:512 * b + C]
-            mm(o, e, ep, T.qf[:, 0:C], T.pf[:, 0:C], True, False, ["eq", "qf"], ["psb%d" % b])
-            mm(o, e, ep, lq[:, 0:C], lp[:, 0:C], False, True, ["eq", "lq%d" % k], ["psb%d" % b])
+            mm(o, e, ep, T.qf[:, 0:C], T.pf[:, 0:C], True, False, ["eq%d" % b, "qf"], ["psb%d" % b])
+            mm(o, e, ep, lq[:, 0:C], lp[:, 0:C], False, True, ["eq%d" % b, "lq%d" % k], ["psb%d" % b])
 
         def meet(b):
             act(T.zf[:, C * b:C * b + C], T.psb[:, 512 * b:512 * b + C], ["psb%d" % b], ["zf%d" % b], 0.5)
 
-        def hop(out, w, window, reads, off, oname, c0):
-            tcopy(out[:, 0:128], window.indirect(off[:, c0:c0 + 8]), reads + [oname], [w + ".v"])
-            act(out[:, 128:C], window.indirect(off[:, c0 + 8:c0 + 16]), reads + [oname], [w + ".s"])
-
-        ttt(T.t1[:], sl[:], T.en[:], A.mult, ["sl%d" % k, "en"], ["t1"])
-        ttt(T.ts[:, 0:16], T.t1[:], T.ea[:], A.add, ["t1", "ea"], ["ts0"])
-        ttt(T.ts[:, 16:32], T.ea[:], T.t1[:], A.subtract, ["t1", "ea"], ["ts1"])
-        tcopy(T.t0[:], T.ts[:], ["ts0", "ts1"], ["t0"])
+        op("v", lambda: V.tensor_tensor_scan(T.ts[:], sl[:], T.pk[:], 0.0, A.mult, A.add), ["sl%d" % k, "pk0", "pk1", "pk2"], ["ts"])
+        tcopy(T.t0[:, 0:16], T.ts[:, 1:48:3], ["ts"], ["t0"])
+        spare.append(lambda: tcopy(T.t0[:, 16:32], T.ts[:, 2:48:3], ["ts"], ["t0e"]))
+        if k == 0:
+            for n in ("st1", "st2"):
+                spare.append(lambda n=n: fill(T[n][:], -1.0, [n]))
+                spare.append(lambda n=n: fill(T[n][:, 0:48:3], 0.0, [n]))
+            spare.append(lambda: quant(T.vq[:, 0:128], T.vp[:, 0:128], T.vt[:, 0:512], ["vt"], ["vq"]))
         hop(T.wa, "wa", T.wi[:, 0:512], ["wi"], T.t0, "t0", 0)
-        off, oname, c0 = T.t0, "t0", 0
-        for i in range(8):
-            a, b = i % 2, 1 - i % 2
-            hop(win[b], wn[b], win[a][:, 0:512], [wn[a] + ".v", wn[a] + ".s", wn[a] + ".k"], off, oname, c0)
-            if i < 7:
-                if i >= 4:
-                    meet(i - 4)
-                scan_to(T.tt[:, 16 * i:16 * i + 16], win[b][:, 0:C], 256.25, [wn[b] + ".v", wn[b] + ".s"], ["tt%d" % i])
+        off, oname, c0, a = T.t0, "t0", 0, 0
+        for i in range(4):
+            for _ in range(3):
+                hop(win[1 - a], wn[1 - a], win[a][:, 0:512], [wn[a] + ".v", wn[a] + ".s", wn[a] + ".k"], off, oname, c0)
+                a = 1 - a
+            if i < 3:
+                if i > 0:
+                    meet(2 * i - 2)
+                    meet(2 * i - 1)
+                scan(win[a][:, 0:C], [wn[a] + ".v", wn[a] + ".s"])
+                table(T.tt[:, 16 * i:16 * i + 16], 256.25, ["tt%d" % i])
                 off, oname, c0 = T.tt, "tt%d" % i, 16 * i
-        hop(T.ar, "ar", T.wa[:, 0:512], ["wa.v", "wa.s", "wa.k"], T.t0, "t0", 16)
-        meet(3)
-        scan_to(T.at[:], T.ar[:], 0.25, ["ar.v", "ar.s"], ["at"])
-        act(rr[:], frow[:, 0:C].indirect(T.at[:, 0:16]), [frname, "at"], ["rr%d" % k])
+        hop(T.ar, "ar", win[a][:, 0:512], [wn[a] + ".v", wn[a] + ".s", wn[a] + ".k"], T.t0, "t0e", 16)
+        scan(T.ar[:, 0:C], ["ar.v", "ar.s"])
+        table(T.at[:], 0.25, ["at"])
+
+        def list_row():
+            act(rr[:], frow[:, 0:C].indirect(T.at[:, 0:16]), [frname, "at"], ["rr%d" % k])
+
+        if k == 0:
+            list_row()
         for b in range(4):
             f = tcopy if b == 0 else act
             f(T.zt[:, b:1024:4], T.zf[:, C * b:C * b + C].indirect(T.at[:, 0:16]), ["zf%d" % b, "at"], ["zt%d" % b])
-        scan_to(rt[:], rr[:], 0.25, ["rr%d" % k], ["rt%d" % k])
+        if k == 0:
+            scan(rr[:], ["rr%d" % k], "scr")
+            table(rt[:], 0.25, ["rt%d" % k], "scr")
+            tcopy(T.ir[:, 0:C].indirect(rt[:, 0:16]), T.wi[:, C:2 * C], ["wi", "rt%d" % k], ["ir"])
+            quant(T.qz[:, 0:C], T.pz[:, 0:C], T.zt[:, 0:1024], ["zt%d" % b for b in range(4)], ["qz"])
+            scan(T.ir[:, 0:C], ["ir"])
+            table(it[:], 0.25, ["it%d" % k])
+        else:
+            tcopy(T.ir[:, 0:C].indirect(T.at[:, 0:16]), T.wi[:, C:2 * C], ["wi", "at"], ["ir"])
+            quant(T.qz[:, 0:C], T.pz[:, 0:C], T.zt[:, 0:1024], ["zt%d" % b for b in range(4)], ["qz"])
+            hop(T.iv, "iv", T.ir[:, 0:C], ["ir"], T["it%d" % (k - 1)], "it%d" % (k - 1), 0)
+            list_row()
+            scan(T.iv[:, 0:C], ["iv.v", "iv.s"])
+            if k < 2:
+                scan(rr[:], ["rr%d" % k], "scr")
+            table(it[:], 0.25, ["it%d" % k])
+            if k < 2:
+                table(rt[:], 0.25, ["rt%d" % k], "scr")
         if k < 2:
             nd = T.cores[rank ^ ROUNDS[k + 1]]
             send(nd, T["el%d" % (k + 1)][:], rt[:], "ar_l%d" % (k + 1), ["rt%d" % k])
             arrives("ar_l%d" % (k + 1), len(topo.engines(nd, core)), ["el%d" % (k + 1)])
-        tcopy(T.ir[:, 0:C].indirect(rt[:, 0:16]), T.wi[:, C:2 * C], ["wi", "rt%d" % k], ["ir"])
-        quant(T.qz[:, 0:C], T.pz[:, 0:C], T.zt[:, 0:1024], ["zt%d" % b for b in range(4)], ["qz"])
-        scan_to(T.it[:], T.ir[:], 0.25, ["ir"], ["it"])
         for b in range(4):
             mm(T.psb[:, 512 * b:512 * b + C], T.wq[:, 128 * b:128 * b + 128], T.wp[:, 128 * b:128 * b + 128], T.qz[:, 0:C], T.pz[:, 0:C], True, True,
                ["wq", "wp", "qz"], ["psb%d" % b])
         xn = T["xt%d" % (k + 1)]
         for b in range(4):
             act(T.pb[:, C * b:C * b + C], T.psb[:, 512 * b:512 * b + C], ["psb%d" % b], ["pb%d" % b], 0.015625)
-            ttt(xn[:, b:1024:4], T.pb[:, C * b:C * b + C].indirect(T.it[:, 0:16]), T.fh[:, C * b:C * b + C], A.add,
-                ["pb%d" % b, "it", "fh%d" % b], ["xt%d.%d" % (k + 1, b)])
+            ttt(xn[:, b:1024:4], T.pb[:, C * b:C * b + C].indirect(it[:, 0:16]), T.fh[:, C * b:C * b + C], A.add,
+                ["pb%d" % b, "it%d" % k, "fh%d" % b], ["xt%d.%d" % (k + 1, b)])
     act(T.lnf[:], T.rr2[:], ["rr2"], ["lnf"])
     op("y", lambda: g.sync.dma_start(T.ln[:], T.lnf[0:128:16, :]), ["lnf"], ["ln"], "out", 16)
     quant(T.qx3[:, 0:C], T.px3[:, 0:C], T.xt3[:, 0:1024], ["xt3.%d" % b for b in range(4)], ["qx3"])

@@ -4,7 +4,7 @@ C = 256
 ROUNDS = (1, 2, 4)
 COPY = ActivationFunctionType.Copy
 IDENTITY = ActivationFunctionType.Identity
-LIFT = 16384.0
+LIFT = 65536.0
 CODES = "float8_e4m3fn_x4"
 
 SCRATCH = {
@@ -24,7 +24,7 @@ SCRATCH = {
     "k1": ("sbuf", [128, C], "float32"), "sc0": ("sbuf", [128, 1], "float32"), "scc": ("sbuf", [128, 1], "float32"),
     "pq": ("sbuf", [128, 16], "int32"), "pq2": ("sbuf", [128, 16], "int32"), "cj": ("sbuf", [128, 16], "float32"),
     "jj": ("sbuf", [128, 16], "float32"), "jh": ("sbuf", [128, 16], "float32"), "oi": ("sbuf", [128, 8], "int32"), "ou": ("sbuf", [128, 8], "uint16"),
-    "mb": ("sbuf", [128, C], "bfloat16"), "ms": ("sbuf", [128, C], "bfloat16"), "scn": ("sbuf", [128, C], "float32"), "scr": ("sbuf", [128, C], "float32"),
+    "mb": ("sbuf", [128, C], "bfloat16"), "ms": ("sbuf", [128, C], "bfloat16"), "scn": ("sbuf", [128, C], "bfloat16"), "scr": ("sbuf", [128, C], "bfloat16"),
     "eh": ("sbuf", [128, 16], "float32"), "ed": ("sbuf", [128, 16], "float32"),
     "pk": ("sbuf", [128, 48], "float32"), "ts": ("sbuf", [128, 48], "float32"), "t0": ("sbuf", [128, 32], "uint16"),
     "tt": ("sbuf", [128, 48], "uint16"), "wa": ("sbuf", [128, 512], "bfloat16"), "wb": ("sbuf", [128, 512], "bfloat16"),
@@ -149,16 +149,16 @@ def rank_program(g, core, T, topo):
     A = AluOpType
 
     def scan(row, r, w="scn"):
-        op("v", lambda: V.tensor_tensor_scan(T[w][:, 0:C], T.cu[:, 0:C], row, 0.0, A.mult, A.add), r + ["cu"], [w])
+        op("v", lambda: V.tensor_tensor_scan(T[w][:, 0:C], T.cu[:, 0:C], row[:, 0:C], 0.0, A.mult, A.add), r + ["cu"], [w])
 
     def table(out, bias, w, s="scn"):
         tts(out, T[s][:, 15:C:16], T.scc[:, 0:1], bias, A.mult, A.add, [s, "scc"], w)
 
     spare = []
 
-    def hop(out, w, window, reads, off, oname, c0):
-        tcopy(out[:, 0:128], window.indirect(off[:, c0:c0 + 8]), reads + [oname], [w + ".v"])
-        act(out[:, 128:C], window.indirect(off[:, c0 + 8:c0 + 16]), reads + [oname], [w + ".s"])
+    def hop(out, w, window, reads, off, oname, c0, n=8):
+        act(out[:, 0:16 * n], window.indirect(off[:, c0:c0 + n]), reads + [oname], [w + ".s"])
+        tcopy(out[:, 16 * n:C], window.indirect(off[:, c0 + n:c0 + 16]), reads + [oname], [w + ".v"])
         if spare:
             spare.pop(0)()
 
@@ -178,23 +178,22 @@ def rank_program(g, core, T, topo):
     first = T.cores[rank ^ ROUNDS[0]]
     send(first, T.el0[:], T.flb[:], "ar_l0", ["flb"])
     arrives("ar_l0", len(topo.engines(first, core)), ["el0"])
-    fill(T.st0[:], -1.0, ["st0"])
-    fill(T.st0[:, 0:48:3], 0.0, ["st0"])
     tts(T.jm2[:], T.jm[:], 15, None, A.bitwise_and, None, ["jm"], ["jm2"])
     tcopy(T.ou[:], T.oi[:], ["oi"], ["ou"])
+    fill(T.st0[:], -1.0, ["st0"])
     tts(T.thr[:], T.jm2[:], 0.0, 1.0e29, A.not_equal, A.mult, ["jm2"], ["thr"])
     tts(T.rst[:], T.jm2[:], 0.0, None, A.not_equal, None, ["jm2"], ["rst"])
-    tts(T.k1[:], T.jm2[:], 1.0, LIFT - 1.0, A.is_equal, A.mult, ["jm2"], ["k1"])
+    fill(T.st0[:, 0:48:3], 0.0, ["st0"])
     tts(T.sc0[:], T.jm2[:, 15:16], 0.0, 1.0 - 1.0 / LIFT, A.is_equal, A.mult, ["jm2"], ["sc0"])
     tts(T.pq2[:], T.pq[:], 15, None, A.bitwise_and, None, ["pq"], ["pq2"])
-    ttt(T.cu[:], T.k1[:], T.rst[:], A.add, ["k1", "rst"], ["cu"])
     tts(T.scc[:], T.sc0[:], 1.0 / LIFT, None, A.add, None, ["sc0"], ["scc"])
     ttt(T.jj[:], T.pq2[:], T.cj[:], A.add, ["pq2", "cj"], ["jj"])
+    tcopy(T.ft[:], T.flb[:], ["flb"], ["ft"])
+    tts(T.k1[:], T.jm2[:], 1.0, LIFT - 1.0, A.is_equal, A.mult, ["jm2"], ["k1"])
     quant(T.uq[:, 0:128], T.up[:, 0:128], T.ut[:, 0:512], ["ut"], ["uq"])
     tts(T.jh[:], T.jj[:], 0.5, None, A.mult, None, ["jj"], ["jh"])
     op("v", lambda: V.tensor_copy(T.urq[:, 0:128].bitcast(dt.uint32), T.uq[:, 0:128].bitcast(dt.uint32).indirect(T.ou[:, 0:8])), ["uq", "ou"], ["urq"])
-    tcopy(T.urp[:, 0:128], T.up[:, 0:128].indirect(T.ou[:, 0:8]), ["uq", "ou"], ["urp"])
-    tcopy(T.ft[:], T.flb[:], ["flb"], ["ft"])
+    act(T.urp[:, 0:128], T.up[:, 0:128].indirect(T.ou[:, 0:8]), ["uq", "ou"], ["urp"])
     op("s", lambda: S.activation(T.ia[:], T.ie[:], ActivationFunctionType.Abs), ["ie"], ["ia"])
     op("s", lambda: S.activation(T.ew[:], T.ia[:], ActivationFunctionType.Relu, bias=1.0, scale=-1.0), ["ia"], ["ew"])
     op("s", lambda: S.activation(T.wi[:], T.ie[:, 0:512], IDENTITY, bias=T.wcol[:, 0:1]), ["ie", "wcol"], ["wi"])
@@ -210,18 +209,22 @@ def rank_program(g, core, T, topo):
         lq, lp, st, sl, el = T["lq%d" % k], T["lp%d" % k], T["st%d" % k], T["sl%d" % k], T["el%d" % k]
         rr, rt, it = T["rr%d" % k], T["rt%d" % k], T["it%d" % k]
         Xt = ["xt%d.%d" % (k, b) for b in range(4)]
-        quant(qx[:, 0:C], px[:, 0:C], xt[:, 0:1024], Xt, ["qx%d" % k])
+        Qx = ["qx%d.0" % k, "qx%d.1" % k]
         for h in range(2):
-            mm(T.psb[:, 512 * h:512 * h + 128], T.urq[:, 0:128], T.urp[:, 0:128], qx[:, 128 * h:128 * h + 128], px[:, 128 * h:128 * h + 128], True, True,
-               ["urq", "urp", "qx%d" % k], ["psb%d" % h])
+            c = 128 * h
+            quant(qx[:, c:c + 128], px[:, c:c + 128], xt[:, 4 * c:4 * c + 512], Xt, [Qx[h]])
+            mm(T.psb[:, 4 * c:4 * c + 128], T.urq[:, 0:128], T.urp[:, 0:128], qx[:, c:c + 128], px[:, c:c + 128], True, True, ["urq", "urp", Qx[h]], ["psb%d" % h])
         for h in range(2):
-            ttt(T.mb[:, 128 * h:128 * h + 128], T.psb[:, 512 * h:512 * h + 128], T.thr[:, 128 * h:128 * h + 128], A.is_gt, ["psb%d" % h, "thr"], ["mb%d" % h])
-        op("v", lambda: V.tensor_tensor_scan(T.ms[:], T.rst[:], T.mb[:], 0.0, A.mult, A.add), ["rst", "mb0", "mb1"], ["ms"])
-        tts(st[:, 1:48:3], T.ms[:, 15:C:16], 2.0, -1.0, A.mult, A.add, ["ms"], ["st%d" % k])
+            c = 128 * h
+            ttt(T.mb[:, c:c + 128], T.psb[:, 4 * c:4 * c + 128], T.thr[:, c:c + 128], A.is_gt, ["psb%d" % h, "thr"], ["mb%d" % h])
+        for h in range(2):
+            op("v", lambda c=128 * h: V.tensor_tensor_scan(T.ms[:, c:c + 128], T.rst[:, c:c + 128], T.mb[:, c:c + 128], 0.0, A.mult, A.add),
+               ["rst", "mb%d" % h], ["ms%d" % h])
+        tts(st[:, 1:48:3], T.ms[:, 15:C:16], 2.0, -1.0, A.mult, A.add, ["ms0", "ms1"], ["st%d" % k])
         send(d, sl[:], st[:], "ar_s%d" % k, ["st%d" % k])
         arrives("ar_s%d" % k, ne, ["sl%d" % k])
-        send(d, lq[:, 0:C].bitcast(dt.uint8), qx[:, 0:C].bitcast(dt.uint8), "ar_d%d" % k, ["qx%d" % k])
-        send(d, lp[:, 0:C], px[:, 0:C], "ar_d%d" % k, ["qx%d" % k])
+        send(d, lq[:, 0:C].bitcast(dt.uint8), qx[:, 0:C].bitcast(dt.uint8), "ar_d%d" % k, Qx)
+        send(d, lp[:, 0:C], px[:, 0:C], "ar_d%d" % k, Qx)
         arrives("ar_d%d" % k, 2 * ne, ["lq%d" % k])
         fsrc, fname = (T.ft, "ft") if k == 0 else (T["rt%d" % (k - 1)], "rt%d" % (k - 1))
         frow, frname = (T.fr, "fr") if k == 0 else (T["rr%d" % (k - 1)], "rr%d" % (k - 1))
@@ -235,30 +238,45 @@ def rank_program(g, core, T, topo):
         if k == 0:
             for b in range(4):
                 quant(T.eq[:, 128 * b:128 * b + 128], T.ep[:, 128 * b:128 * b + 128], T.ew[:, 4 - b:516 - b], ["ew"], ["eq%d" % b])
-            act(T.fr[:], T.wi[:, C:2 * C].indirect(T.ft[:, 0:16]), ["wi", "ft"], ["fr"])
         tts(T.eh[:], el[:], 0.5, None, A.mult, None, ["el%d" % k], ["eh"])
+        if k == 0:
+            ttt(T.cu[:], T.k1[:], T.rst[:], A.add, ["k1", "rst"], ["cu"])
         ttt(T.ed[:], T.eh[:], T.jh[:], A.subtract, ["eh", "jh"], ["ed"])
         ttt(T.pk[:, 1:48:3], T.eh[:], T.jh[:], A.add, ["eh", "jh"], ["pk1"])
         ttt(T.pk[:, 0:48:3], T.ed[:], st[:, 1:48:3], A.mult, ["ed", "st%d" % k], ["pk0"])
         tts(T.pk[:, 2:48:3], T.pk[:, 1:48:3], 2.0, None, A.mult, None, ["pk1"], ["pk2"])
-        quant(T.qf[:, 0:C], T.pf[:, 0:C], T.xf[:, 0:1024], ["xf%d" % b for b in range(4)], ["qf"])
         for b in range(4):
             mm(T.psa[:, 512 * b:512 * b + C], T.eq[:, 128 * b:128 * b + 128], T.ep[:, 128 * b:128 * b + 128], qx[:, 0:C], px[:, 0:C], True, True,
-               ["eq%d" % b, "qx%d" % k], ["psa%d" % b])
-        for b in range(4):
+               ["eq%d" % b] + Qx, ["psa%d" % b])
+
+        def quant_f(h):
+            c = 128 * h
+            quant(T.qf[:, c:c + 128], T.pf[:, c:c + 128], T.xf[:, 4 * c:4 * c + 512], ["xf%d" % b for b in range(4)], ["qf%d" % h])
+
+        def meet_products():
+            for b in range(4):
+                e, ep, o = T.eq[:, 128 * b:128 * b + 128], T.ep[:, 128 * b:128 * b + 128], T.psb[:, 512 * b:512 * b + C]
+                mm(o, e, ep, T.qf[:, 0:C], T.pf[:, 0:C], True, False, ["eq%d" % b, "qf0", "qf1"], ["psb%d" % b])
+                mm(o, e, ep, lq[:, 0:C], lp[:, 0:C], False, True, ["eq%d" % b, "lq%d" % k], ["psb%d" % b])
+
+        def half(b):
             act(T.fh[:, C * b:C * b + C], T.psa[:, 512 * b:512 * b + C], ["psa%d" % b], ["fh%d" % b], 0.5)
-        for b in range(4):
-            e, ep, o = T.eq[:, 128 * b:128 * b + 128], T.ep[:, 128 * b:128 * b + 128], T.psb[:, 512 * b:512 * b + C]
-            mm(o, e, ep, T.qf[:, 0:C], T.pf[:, 0:C], True, False, ["eq%d" % b, "qf"], ["psb%d" % b])
-            mm(o, e, ep, lq[:, 0:C], lp[:, 0:C], False, True, ["eq%d" % b, "lq%d" % k], ["psb%d" % b])
 
         def meet(b):
             act(T.zf[:, C * b:C * b + C], T.psb[:, 512 * b:512 * b + C], ["psb%d" % b], ["zf%d" % b], 0.5)
 
+        if k > 0:
+            quant_f(0)
+            quant_f(1)
+            meet_products()
+            for b in range(4):
+                half(b)
         op("v", lambda: V.tensor_tensor_scan(T.ts[:], sl[:], T.pk[:], 0.0, A.mult, A.add), ["sl%d" % k, "pk0", "pk1", "pk2"], ["ts"])
         tcopy(T.t0[:, 0:16], T.ts[:, 1:48:3], ["ts"], ["t0"])
         spare.append(lambda: tcopy(T.t0[:, 16:32], T.ts[:, 2:48:3], ["ts"], ["t0e"]))
         if k == 0:
+            spare.append(lambda: quant_f(0))
+            spare.append(lambda: quant_f(1))
             for n in ("st1", "st2"):
                 spare.append(lambda n=n: fill(T[n][:], -1.0, [n]))
                 spare.append(lambda n=n: fill(T[n][:, 0:48:3], 0.0, [n]))
@@ -270,18 +288,41 @@ def rank_program(g, core, T, topo):
                 hop(win[1 - a], wn[1 - a], win[a][:, 0:512], [wn[a] + ".v", wn[a] + ".s", wn[a] + ".k"], off, oname, c0)
                 a = 1 - a
             if i < 3:
-                if i > 0:
-                    meet(2 * i - 2)
-                    meet(2 * i - 1)
-                scan(win[a][:, 0:C], [wn[a] + ".v", wn[a] + ".s"])
+                if i == 0 and k == 0:
+                    meet_products()
+                    half(0)
+                    half(1)
+                if i == 1:
+                    meet(0)
+                    meet(1)
+                if i == 2:
+                    meet(2)
+                    if k == 0:
+                        meet(3)
+                scan(win[a], [wn[a] + ".v", wn[a] + ".s"])
                 table(T.tt[:, 16 * i:16 * i + 16], 256.25, ["tt%d" % i])
                 off, oname, c0 = T.tt, "tt%d" % i, 16 * i
         hop(T.ar, "ar", win[a][:, 0:512], [wn[a] + ".v", wn[a] + ".s", wn[a] + ".k"], T.t0, "t0e", 16)
-        scan(T.ar[:, 0:C], ["ar.v", "ar.s"])
+        if k == 0:
+            act(T.fr[:], T.wi[:, C:2 * C].indirect(T.ft[:, 0:16]), ["wi", "ft"], ["fr"])
+        else:
+            meet(3)
+        scan(T.ar, ["ar.v", "ar.s"])
         table(T.at[:], 0.25, ["at"])
 
         def list_row():
             act(rr[:], frow[:, 0:C].indirect(T.at[:, 0:16]), [frname, "at"], ["rr%d" % k])
+
+        def list_out():
+            table(rt[:], 0.25, ["rt%d" % k], "scr")
+            nd = T.cores[rank ^ ROUNDS[k + 1]]
+            send(nd, T["el%d" % (k + 1)][:], rt[:], "ar_l%d" % (k + 1), ["rt%d" % k])
+            arrives("ar_l%d" % (k + 1), len(topo.engines(nd, core)), ["el%d" % (k + 1)])
+
+        def quant_z():
+            for h in range(2):
+                c = 128 * h
+                quant(T.qz[:, c:c + 128], T.pz[:, c:c + 128], T.zt[:, 4 * c:4 * c + 512], ["zt%d" % b for b in range(4)], ["qz%d" % h])
 
         if k == 0:
             list_row()
@@ -289,45 +330,47 @@ def rank_program(g, core, T, topo):
             f = tcopy if b == 0 else act
             f(T.zt[:, b:1024:4], T.zf[:, C * b:C * b + C].indirect(T.at[:, 0:16]), ["zf%d" % b, "at"], ["zt%d" % b])
         if k == 0:
-            scan(rr[:], ["rr%d" % k], "scr")
-            table(rt[:], 0.25, ["rt%d" % k], "scr")
+            scan(rr, ["rr%d" % k], "scr")
+            list_out()
             tcopy(T.ir[:, 0:C].indirect(rt[:, 0:16]), T.wi[:, C:2 * C], ["wi", "rt%d" % k], ["ir"])
-            quant(T.qz[:, 0:C], T.pz[:, 0:C], T.zt[:, 0:1024], ["zt%d" % b for b in range(4)], ["qz"])
-            scan(T.ir[:, 0:C], ["ir"])
+            quant_z()
+            scan(T.ir, ["ir"])
             table(it[:], 0.25, ["it%d" % k])
         else:
             tcopy(T.ir[:, 0:C].indirect(T.at[:, 0:16]), T.wi[:, C:2 * C], ["wi", "at"], ["ir"])
-            quant(T.qz[:, 0:C], T.pz[:, 0:C], T.zt[:, 0:1024], ["zt%d" % b for b in range(4)], ["qz"])
-            hop(T.iv, "iv", T.ir[:, 0:C], ["ir"], T["it%d" % (k - 1)], "it%d" % (k - 1), 0)
+            quant_z()
+            hop(T.iv, "iv", T.ir[:, 0:C], ["ir"], T["it%d" % (k - 1)], "it%d" % (k - 1), 0, 12)
             list_row()
-            scan(T.iv[:, 0:C], ["iv.v", "iv.s"])
-            if k < 2:
-                scan(rr[:], ["rr%d" % k], "scr")
+            scan(T.iv, ["iv.v", "iv.s"])
             table(it[:], 0.25, ["it%d" % k])
             if k < 2:
-                table(rt[:], 0.25, ["rt%d" % k], "scr")
-        if k < 2:
-            nd = T.cores[rank ^ ROUNDS[k + 1]]
-            send(nd, T["el%d" % (k + 1)][:], rt[:], "ar_l%d" % (k + 1), ["rt%d" % k])
-            arrives("ar_l%d" % (k + 1), len(topo.engines(nd, core)), ["el%d" % (k + 1)])
-        for b in range(4):
-            mm(T.psb[:, 512 * b:512 * b + C], T.wq[:, 128 * b:128 * b + 128], T.wp[:, 128 * b:128 * b + 128], T.qz[:, 0:C], T.pz[:, 0:C], True, True,
-               ["wq", "wp", "qz"], ["psb%d" % b])
+                scan(rr, ["rr%d" % k], "scr")
+        cuts = ((0, 0, 128, T.psb[:, 0:128], "psb0"), (0, 128, C, T.psa[:, 0:128], "psa0")) + tuple(
+            (b, 0, C, T.psb[:, 512 * b:512 * b + C], "psb%d" % b) for b in (1, 2, 3))
+        for b, lo, hi, o, n in cuts:
+            mm(o, T.wq[:, 128 * b:128 * b + 128], T.wp[:, 128 * b:128 * b + 128], T.qz[:, lo:hi], T.pz[:, lo:hi], True, True,
+               ["wq", "wp"] + ["qz%d" % h for h in range(2) if lo <= 128 * h < hi], [n])
+        for b, lo, hi, o, n in cuts:
+            if k == 0 and b > 1:
+                half(b)
+            act(T.pb[:, C * b + lo:C * b + hi], o, [n], ["pb%d.%d" % (b, lo)], 0.015625)
         xn = T["xt%d" % (k + 1)]
         for b in range(4):
-            act(T.pb[:, C * b:C * b + C], T.psb[:, 512 * b:512 * b + C], ["psb%d" % b], ["pb%d" % b], 0.015625)
             ttt(xn[:, b:1024:4], T.pb[:, C * b:C * b + C].indirect(it[:, 0:16]), T.fh[:, C * b:C * b + C], A.add,
-                ["pb%d" % b, "it%d" % k, "fh%d" % b], ["xt%d.%d" % (k + 1, b)])
+                ["pb%d.%d" % (c, lo) for c, lo, hi, o, n in cuts if c == b] + ["it%d" % k, "fh%d" % b], ["xt%d.%d" % (k + 1, b)])
+            if b == 0 and k == 1:
+                list_out()
     act(T.lnf[:], T.rr2[:], ["rr2"], ["lnf"])
     op("y", lambda: g.sync.dma_start(T.ln[:], T.lnf[0:128:16, :]), ["lnf"], ["ln"], "out", 16)
-    quant(T.qx3[:, 0:C], T.px3[:, 0:C], T.xt3[:, 0:1024], ["xt3.%d" % b for b in range(4)], ["qx3"])
+    Q3 = ["qx3.0", "qx3.1"]
     for h in range(2):
-        mm(T.psa[:, 512 * h:512 * h + 128], T.vq[:, 0:128], T.vp[:, 0:128], T.qx3[:, 128 * h:128 * h + 128], T.px3[:, 128 * h:128 * h + 128], True, True,
-           ["vq", "qx3"], ["psa%d" % h])
-    op("y", lambda: g.sync.dma_start(T.oc[:, 0:4 * C], T.qx3[:, 0:C].bitcast(dt.uint8)), ["qx3"], ["oc"], "out", 16)
+        c = 128 * h
+        quant(T.qx3[:, c:c + 128], T.px3[:, c:c + 128], T.xt3[:, 4 * c:4 * c + 512], ["xt3.%d" % b for b in range(4)], [Q3[h]])
+        mm(T.psa[:, 4 * c:4 * c + 128], T.vq[:, 0:128], T.vp[:, 0:128], T.qx3[:, c:c + 128], T.px3[:, c:c + 128], True, True, ["vq", Q3[h]], ["psa%d" % h])
+    op("y", lambda: g.sync.dma_start(T.oc[:, 0:4 * C], T.qx3[:, 0:C].bitcast(dt.uint8)), Q3, ["oc"], "out", 16)
 
     def scales(q, queue, i):
-        op(q, lambda: queue.dma_start(T.osc[4 * i:4 * i + 4, 0:C], T.px3[32 * i:32 * i + 4, 0:C]), ["qx3"], ["osc%d" % i], "out", 16)
+        op(q, lambda: queue.dma_start(T.osc[4 * i:4 * i + 4, 0:C], T.px3[32 * i:32 * i + 4, 0:C]), Q3, ["osc%d" % i], "out", 16)
 
     scales("y", g.sync, 0)
     scales("y", g.sync, 1)

from concourse.mybir import dt, AluOpType, ActivationFunctionType

C = 256
ROUNDS = (1, 2, 4)
COPY = ActivationFunctionType.Copy
IDENTITY = ActivationFunctionType.Identity
LIFT = 65536.0
CODES = "float8_e4m3fn_x4"

SCRATCH = {
    "flb": ("sbuf", [128, 16], "int32"),
    "ft": ("sbuf", [128, 16], "uint16"), "f4": ("sbuf", [128, 64], "uint16"), "fr": ("sbuf", [128, C], "bfloat16"),
    "ut": ("sbuf", [128, 512], "bfloat16"), "uq": ("sbuf", [128, 128], CODES), "up": ("sbuf", [128, 128], "uint8"),
    "urq": ("sbuf", [128, 128], CODES), "urp": ("sbuf", [128, 128], "uint8"),
    "vt": ("sbuf", [128, 512], "bfloat16"), "vq": ("sbuf", [128, 128], CODES), "vp": ("sbuf", [128, 128], "uint8"),
    "wq": ("sbuf", [128, 512], CODES), "wp": ("sbuf", [128, 512], "uint8"),
    "ew": ("sbuf", [128, 516], "bfloat16"), "eq": ("sbuf", [128, 512], CODES), "ep": ("sbuf", [128, 512], "uint8"),
    "xf": ("sbuf", [128, 1024], "bfloat16"), "qf": ("sbuf", [128, C], CODES), "pf": ("sbuf", [128, C], "uint8"),
    "zt": ("sbuf", [128, 1024], "bfloat16"), "qz": ("sbuf", [128, C], CODES), "pz": ("sbuf", [128, C], "uint8"),
    "fh": ("sbuf", [128, 1024], "bfloat16"), "zf": ("sbuf", [128, 1024], "bfloat16"), "pb": ("sbuf", [128, 1024], "float32"),
    "wi": ("sbuf", [128, 512], "bfloat16"), "ie": ("sbuf", [128, 516], "float32"), "ia": ("sbuf", [128, 516], "float32"),
    "wcol": ("sbuf", [128, 1], "float32"), "jm": ("sbuf", [128, C], "int32"), "jm2": ("sbuf", [128, C], "int32"),
    "thr": ("sbuf", [128, C], "float32"), "rst": ("sbuf", [128, C], "bfloat16"), "cu": ("sbuf", [128, C], "bfloat16"),
    "k1": ("sbuf", [128, C], "float32"), "sc0": ("sbuf", [128, 1], "float32"), "scc": ("sbuf", [128, 1], "float32"),
    "pq": ("sbuf", [128, 16], "int32"), "pq2": ("sbuf", [128, 16], "int32"), "cj": ("sbuf", [128, 16], "float32"),
    "jj": ("sbuf", [128, 16], "float32"), "jh": ("sbuf", [128, 16], "float32"), "oi": ("sbuf", [128, 8], "int32"), "ou": ("sbuf", [128, 8], "uint16"),
    "mb": ("sbuf", [128, C], "bfloat16"), "ms": ("sbuf", [128, C], "bfloat16"), "scn": ("sbuf", [128, C], "bfloat16"), "scr": ("sbuf", [128, C], "bfloat16"),
    "eh": ("sbuf", [128, 16], "float32"), "ed": ("sbuf", [128, 16], "float32"),
    "pk": ("sbuf", [128, 48], "float32"), "ts": ("sbuf", [128, 48], "float32"), "t0": ("sbuf", [128, 32], "uint16"),
    "tt": ("sbuf", [128, 48], "uint16"), "wa": ("sbuf", [128, 512], "bfloat16"), "wb": ("sbuf", [128, 512], "bfloat16"),
    "ar": ("sbuf", [128, C], "bfloat16"), "at": ("sbuf", [128, 16], "uint16"),
    "ir": ("sbuf", [128, C], "bfloat16"), "iv": ("sbuf", [128, C], "bfloat16"),
    "lnf": ("sbuf", [128, C], "float32"), "yb": ("sbuf", [128, C], "float32"),
    "psa": ("psum", [128, 2048], "float32"), "psb": ("psum", [128, 2048], "float32"),
    "el0": ("sbuf", [128, 16], "int32"), "el1": ("sbuf", [128, 16], "uint16"), "el2": ("sbuf", [128, 16], "uint16"),
}
for _k in range(4):
    SCRATCH["xt%d" % _k] = ("sbuf", [128, 1024], "bfloat16")
    SCRATCH["qx%d" % _k] = ("sbuf", [128, C], CODES)
    SCRATCH["px%d" % _k] = ("sbuf", [128, C], "uint8")
for _k in range(3):
    SCRATCH["lq%d" % _k] = ("sbuf", [128, C], CODES)
    SCRATCH["lp%d" % _k] = ("sbuf", [128, C], "uint8")
    SCRATCH["st%d" % _k] = ("sbuf", [128, 48], "bfloat16")
    SCRATCH["sl%d" % _k] = ("sbuf", [128, 48], "bfloat16")
    SCRATCH["rr%d" % _k] = ("sbuf", [128, C], "bfloat16")
    SCRATCH["rt%d" % _k] = ("sbuf", [128, 16], "uint16")
    SCRATCH["it%d" % _k] = ("sbuf", [128, 16], "uint16")
SEMAPHORES = (["cv", "cs", "cp", "cg", "lo", "lf", "lx", "lu", "lv", "lw", "lws", "out"]
              + ["%s%d" % (a, k) for a in ("ar_s", "ar_l", "ar_d") for k in range(3)])


def rank_program(g, core, T, topo):
    rank = T.rank_of(core)
    if rank is None:
        return
    V, S, P = g.vector, g.scalar, g.tensor
    queues = {"v": V, "s": S, "p": P, "g": g, "y": g.sync}
    own = {"v": "cv", "s": "cs", "p": "cp", "g": "cg"}
    known = {q: {} for q in queues}
    snap = {}
    total = {}
    wrote, read = {}, {}

    def covered(k, d):
        return k.get(d[0], 0) >= d[1]

    def wait(q, deps):
        best = {}
        for d in deps:
            if not covered(known[q], d):
                best[d[0]] = max(best.get(d[0], 0), d[1])
        deps = list(best.items())
        for d in deps:
            if any(o != d and covered(snap[o], d) for o in deps):
                continue
            queues[q].wait_ge(T.sem[d[0]], d[1])
        for d in deps:
            known[q][d[0]] = max(known[q].get(d[0], 0), d[1])
            for s, n in snap[d].items():
                known[q][s] = max(known[q].get(s, 0), n)

    def needs(reads, writes):
        deps = [wrote[t] for t in reads]
        for t in writes:
            if t in wrote:
                deps.append(wrote[t])
            deps += read.get(t, [])
        return deps

    def op(q, call, reads, writes, sem=None, inc=1):
        wait(q, needs(reads, writes))
        name = sem or own[q]
        ins = call()
        ins.then_inc(T.sem[name], inc)
        total[name] = total.get(name, 0) + inc
        me = (name, total[name])
        snap[me] = dict(known[q])
        for t in reads:
            read.setdefault(t, []).append(me)
        for t in writes:
            wrote[t], read[t] = me, []

    def arrives(sem, n, tokens):
        total[sem] = total.get(sem, 0) + n
        for t in tokens:
            wrote[t] = (sem, total[sem])
        snap[(sem, total[sem])] = {}

    def send(dst, out, in_, sem, reads):
        wait("g", needs(reads, []))
        rid, pid, _ = topo.addr(dst)
        g.remote_dma(out, in_, T.sem[sem], T.sem.lo, pid, rid, topo.mask(core, dst))
        total["lo"] = total.get("lo", 0) + len(topo.engines(core, dst))

    def tcopy(out, in_, r, w):
        op("v", lambda: V.tensor_copy(out, in_), r, w)

    def tts(out, in0, s1, s2, o0, o1, r, w):
        if o1 is None:
            op("v", lambda: V.tensor_scalar(out, in0, s1, None, o0), r, w)
        else:
            op("v", lambda: V.tensor_scalar(out, in0, s1, s2, o0, o1), r, w)

    def ttt(out, a, b, o, r, w):
        op("v", lambda: V.tensor_tensor(out, a, b, o), r, w)

    def fill(ap, value, w):
        op("v", lambda: V.memset(ap, value), [], w)

    def quant(q, p, t, r, w):
        op("v", lambda: V.quantize_mx(q, p, t), r, w)

    def act(out, in_, r, w, scale=None):
        if scale is None:
            op("s", lambda: S.activation(out, in_, COPY), r, w)
        else:
            op("s", lambda: S.activation(out, in_, COPY, scale=scale), r, w)

    def mm(out, a, ap, b, bp, start, stop, r, w):
        op("p", lambda: P.matmul_mx(out, a, ap, b, bp, start, stop), r, w)

    def iota(out, pattern, base, cm, w, small=False):
        if small:
            op("g", lambda: g.iota(out, pattern, base, cm, allow_small_or_imprecise_dtypes=True), [], w)
        else:
            op("g", lambda: g.iota(out, pattern, base, cm), [], w)

    A = AluOpType

    def scan(row, r, w="scn"):
        op("v", lambda: V.tensor_tensor_scan(T[w][:, 0:C], T.cu[:, 0:C], row[:, 0:C], 0.0, A.mult, A.add), r + ["cu"], [w])

    def table(out, bias, w, s="scn"):
        tts(out, T[s][:, 15:C:16], T.scc[:, 0:1], bias, A.mult, A.add, [s, "scc"], w)

    spare = []

    def hop(out, w, window, reads, off, oname, c0, n=8):
        act(out[:, 0:16 * n], window.indirect(off[:, c0:c0 + n]), reads + [oname], [w + ".s"])
        tcopy(out[:, 16 * n:C], window.indirect(off[:, c0 + n:c0 + 16]), reads + [oname], [w + ".v"])
        if spare:
            spare.pop(0)()

    op("s", lambda: S.dma_start(T.flb[:], T.fl[:]), [], ["flb"], "lf", 16)
    op("y", lambda: g.sync.dma_start(T.xt0[:], T.x[:]), [], ["xt0.%d" % b for b in range(4)], "lx", 16)
    op("s", lambda: S.dma_start(T.ut[:], T.u[:]), [], ["ut"], "lu", 16)
    wait("y", [wrote["xt0.0"]])
    op("y", lambda: g.sync.dma_start(T.wq[:, 0:512].bitcast(dt.uint8), T.wc[:]), [], ["wq"], "lw", 16)
    op("y", lambda: g.sync.dma_start(T.wp[:, 0:512], T.ws[:]), [], ["wp"], "lws", 16)
    op("y", lambda: g.sync.dma_start(T.vt[:], T.v[:]), [], ["vt"], "lv", 16)
    iota(T.jm[:], [[1, C]], 0, -1, ["jm"])
    iota(T.oi[:], [[16, 8]], 0, 0, ["oi"])
    iota(T.pq[:], [[0, 16]], 0, 1, ["pq"])
    iota(T.cj[:], [[16, 16]], 256, 0, ["cj"], True)
    iota(T.wcol[:], [[0, 1]], -252, 4, ["wcol"], True)
    iota(T.ie[:], [[1, 516]], -4, -4, ["ie"], True)
    first = T.cores[rank ^ ROUNDS[0]]
    send(first, T.el0[:], T.flb[:], "ar_l0", ["flb"])
    arrives("ar_l0", len(topo.engines(first, core)), ["el0"])
    tts(T.jm2[:], T.jm[:], 15, None, A.bitwise_and, None, ["jm"], ["jm2"])
    tcopy(T.ou[:], T.oi[:], ["oi"], ["ou"])
    fill(T.st0[:], -1.0, ["st0"])
    tts(T.thr[:], T.jm2[:], 0.0, 1.0e29, A.not_equal, A.mult, ["jm2"], ["thr"])
    tts(T.rst[:], T.jm2[:], 0.0, None, A.not_equal, None, ["jm2"], ["rst"])
    fill(T.st0[:, 0:48:3], 0.0, ["st0"])
    tts(T.sc0[:], T.jm2[:, 15:16], 0.0, 1.0 - 1.0 / LIFT, A.is_equal, A.mult, ["jm2"], ["sc0"])
    tts(T.pq2[:], T.pq[:], 15, None, A.bitwise_and, None, ["pq"], ["pq2"])
    tts(T.scc[:], T.sc0[:], 1.0 / LIFT, None, A.add, None, ["sc0"], ["scc"])
    ttt(T.jj[:], T.pq2[:], T.cj[:], A.add, ["pq2", "cj"], ["jj"])
    tcopy(T.ft[:], T.flb[:], ["flb"], ["ft"])
    tts(T.k1[:], T.jm2[:], 1.0, LIFT - 1.0, A.is_equal, A.mult, ["jm2"], ["k1"])
    quant(T.uq[:, 0:128], T.up[:, 0:128], T.ut[:, 0:512], ["ut"], ["uq"])
    tts(T.jh[:], T.jj[:], 0.5, None, A.mult, None, ["jj"], ["jh"])
    op("v", lambda: V.tensor_copy(T.urq[:, 0:128].bitcast(dt.uint32), T.uq[:, 0:128].bitcast(dt.uint32).indirect(T.ou[:, 0:8])), ["uq", "ou"], ["urq"])
    act(T.urp[:, 0:128], T.up[:, 0:128].indirect(T.ou[:, 0:8]), ["uq", "ou"], ["urp"])
    op("s", lambda: S.activation(T.ia[:], T.ie[:], ActivationFunctionType.Abs), ["ie"], ["ia"])
    op("s", lambda: S.activation(T.ew[:], T.ia[:], ActivationFunctionType.Relu, bias=1.0, scale=-1.0), ["ia"], ["ew"])
    op("s", lambda: S.activation(T.wi[:], T.ie[:, 0:512], IDENTITY, bias=T.wcol[:, 0:1]), ["ie", "wcol"], ["wi"])
    act(T.wa[:, C:2 * C], T.wi[:, C:2 * C], ["wi"], ["wa.k"])
    act(T.wb[:, C:2 * C], T.wi[:, C:2 * C], ["wi"], ["wb.k"])

    win = (T.wa, T.wb)
    wn = ("wa", "wb")
    for k, m in enumerate(ROUNDS):
        d = T.cores[rank ^ m]
        ne = len(topo.engines(d, core))
        xt, qx, px = T["xt%d" % k], T["qx%d" % k], T["px%d" % k]
        lq, lp, st, sl, el = T["lq%d" % k], T["lp%d" % k], T["st%d" % k], T["sl%d" % k], T["el%d" % k]
        rr, rt, it = T["rr%d" % k], T["rt%d" % k], T["it%d" % k]
        Xt = ["xt%d.%d" % (k, b) for b in range(4)]
        Qx = ["qx%d.0" % k, "qx%d.1" % k]
        for h in range(2):
            c = 128 * h
            quant(qx[:, c:c + 128], px[:, c:c + 128], xt[:, 4 * c:4 * c + 512], Xt, [Qx[h]])
            mm(T.psb[:, 4 * c:4 * c + 128], T.urq[:, 0:128], T.urp[:, 0:128], qx[:, c:c + 128], px[:, c:c + 128], True, True, ["urq", "urp", Qx[h]], ["psb%d" % h])
        for h in range(2):
            c = 128 * h
            ttt(T.mb[:, c:c + 128], T.psb[:, 4 * c:4 * c + 128], T.thr[:, c:c + 128], A.is_gt, ["psb%d" % h, "thr"], ["mb%d" % h])
        for h in range(2):
            op("v", lambda c=128 * h: V.tensor_tensor_scan(T.ms[:, c:c + 128], T.rst[:, c:c + 128], T.mb[:, c:c + 128], 0.0, A.mult, A.add),
               ["rst", "mb%d" % h], ["ms%d" % h])
        tts(st[:, 1:48:3], T.ms[:, 15:C:16], 2.0, -1.0, A.mult, A.add, ["ms0", "ms1"], ["st%d" % k])
        send(d, sl[:], st[:], "ar_s%d" % k, ["st%d" % k])
        arrives("ar_s%d" % k, ne, ["sl%d" % k])
        send(d, lq[:, 0:C].bitcast(dt.uint8), qx[:, 0:C].bitcast(dt.uint8), "ar_d%d" % k, Qx)
        send(d, lp[:, 0:C], px[:, 0:C], "ar_d%d" % k, Qx)
        arrives("ar_d%d" % k, 2 * ne, ["lq%d" % k])
        fsrc, fname = (T.ft, "ft") if k == 0 else (T["rt%d" % (k - 1)], "rt%d" % (k - 1))
        frow, frname = (T.fr, "fr") if k == 0 else (T["rr%d" % (k - 1)], "rr%d" % (k - 1))
        lay = ((1, 2, 3), (0,)) if k == 0 else ((2, 3), (0, 1))
        for b in lay[0] + lay[1]:
            tts(T.f4[:, 16 * b:16 * b + 16], fsrc[:], 4.0, float(b), A.mult, A.add, [fname], ["f4.%d" % b])
        for b in lay[0]:
            act(T.xf[:, b:1024:4], xt[:, 0:1024].indirect(T.f4[:, 16 * b:16 * b + 16]), Xt + ["f4.%d" % b], ["xf%d" % b])
        for b in lay[1]:
            tcopy(T.xf[:, b:1024:4], xt[:, 0:1024].indirect(T.f4[:, 16 * b:16 * b + 16]), Xt + ["f4.%d" % b], ["xf%d" % b])
        if k == 0:
            for b in range(4):
                quant(T.eq[:, 128 * b:128 * b + 128], T.ep[:, 128 * b:128 * b + 128], T.ew[:, 4 - b:516 - b], ["ew"], ["eq%d" % b])
        tts(T.eh[:], el[:], 0.5, None, A.mult, None, ["el%d" % k], ["eh"])
        if k == 0:
            ttt(T.cu[:], T.k1[:], T.rst[:], A.add, ["k1", "rst"], ["cu"])
        ttt(T.ed[:], T.eh[:], T.jh[:], A.subtract, ["eh", "jh"], ["ed"])
        ttt(T.pk[:, 1:48:3], T.eh[:], T.jh[:], A.add, ["eh", "jh"], ["pk1"])
        ttt(T.pk[:, 0:48:3], T.ed[:], st[:, 1:48:3], A.mult, ["ed", "st%d" % k], ["pk0"])
        tts(T.pk[:, 2:48:3], T.pk[:, 1:48:3], 2.0, None, A.mult, None, ["pk1"], ["pk2"])
        for b in range(4):
            mm(T.psa[:, 512 * b:512 * b + C], T.eq[:, 128 * b:128 * b + 128], T.ep[:, 128 * b:128 * b + 128], qx[:, 0:C], px[:, 0:C], True, True,
               ["eq%d" % b] + Qx, ["psa%d" % b])

        def quant_f(h):
            c = 128 * h
            quant(T.qf[:, c:c + 128], T.pf[:, c:c + 128], T.xf[:, 4 * c:4 * c + 512], ["xf%d" % b for b in range(4)], ["qf%d" % h])

        def meet_products():
            for b in range(4):
                e, ep, o = T.eq[:, 128 * b:128 * b + 128], T.ep[:, 128 * b:128 * b + 128], T.psb[:, 512 * b:512 * b + C]
                mm(o, e, ep, T.qf[:, 0:C], T.pf[:, 0:C], True, False, ["eq%d" % b, "qf0", "qf1"], ["psb%d" % b])
                mm(o, e, ep, lq[:, 0:C], lp[:, 0:C], False, True, ["eq%d" % b, "lq%d" % k], ["psb%d" % b])

        def half(b):
            act(T.fh[:, C * b:C * b + C], T.psa[:, 512 * b:512 * b + C], ["psa%d" % b], ["fh%d" % b], 0.5)

        def meet(b):
            act(T.zf[:, C * b:C * b + C], T.psb[:, 512 * b:512 * b + C], ["psb%d" % b], ["zf%d" % b], 0.5)

        if k > 0:
            quant_f(0)
            quant_f(1)
            meet_products()
            for b in range(4):
                half(b)
        op("v", lambda: V.tensor_tensor_scan(T.ts[:], sl[:], T.pk[:], 0.0, A.mult, A.add), ["sl%d" % k, "pk0", "pk1", "pk2"], ["ts"])
        tcopy(T.t0[:, 0:16], T.ts[:, 1:48:3], ["ts"], ["t0"])
        spare.append(lambda: tcopy(T.t0[:, 16:32], T.ts[:, 2:48:3], ["ts"], ["t0e"]))
        if k == 0:
            spare.append(lambda: quant_f(0))
            spare.append(lambda: quant_f(1))
            for n in ("st1", "st2"):
                spare.append(lambda n=n: fill(T[n][:], -1.0, [n]))
                spare.append(lambda n=n: fill(T[n][:, 0:48:3], 0.0, [n]))
            spare.append(lambda: quant(T.vq[:, 0:128], T.vp[:, 0:128], T.vt[:, 0:512], ["vt"], ["vq"]))
        hop(T.wa, "wa", T.wi[:, 0:512], ["wi"], T.t0, "t0", 0)
        off, oname, c0, a = T.t0, "t0", 0, 0
        for i in range(4):
            for _ in range(3):
                hop(win[1 - a], wn[1 - a], win[a][:, 0:512], [wn[a] + ".v", wn[a] + ".s", wn[a] + ".k"], off, oname, c0)
                a = 1 - a
            if i < 3:
                if i == 0 and k == 0:
                    meet_products()
                    half(0)
                    half(1)
                if i == 1:
                    meet(0)
                    meet(1)
                if i == 2:
                    meet(2)
                    if k == 0:
                        meet(3)
                scan(win[a], [wn[a] + ".v", wn[a] + ".s"])
                table(T.tt[:, 16 * i:16 * i + 16], 256.25, ["tt%d" % i])
                off, oname, c0 = T.tt, "tt%d" % i, 16 * i
        hop(T.ar, "ar", win[a][:, 0:512], [wn[a] + ".v", wn[a] + ".s", wn[a] + ".k"], T.t0, "t0e", 16)
        if k == 0:
            act(T.fr[:], T.wi[:, C:2 * C].indirect(T.ft[:, 0:16]), ["wi", "ft"], ["fr"])
        else:
            meet(3)
        scan(T.ar, ["ar.v", "ar.s"])
        table(T.at[:], 0.25, ["at"])

        def list_row():
            act(rr[:], frow[:, 0:C].indirect(T.at[:, 0:16]), [frname, "at"], ["rr%d" % k])

        def list_out():
            table(rt[:], 0.25, ["rt%d" % k], "scr")
            nd = T.cores[rank ^ ROUNDS[k + 1]]
            send(nd, T["el%d" % (k + 1)][:], rt[:], "ar_l%d" % (k + 1), ["rt%d" % k])
            arrives("ar_l%d" % (k + 1), len(topo.engines(nd, core)), ["el%d" % (k + 1)])

        def quant_z():
            for h in range(2):
                c = 128 * h
                quant(T.qz[:, c:c + 128], T.pz[:, c:c + 128], T.zt[:, 4 * c:4 * c + 512], ["zt%d" % b for b in range(4)], ["qz%d" % h])

        if k == 0:
            list_row()
        for b in range(4):
            f = tcopy if b == 0 else act
            f(T.zt[:, b:1024:4], T.zf[:, C * b:C * b + C].indirect(T.at[:, 0:16]), ["zf%d" % b, "at"], ["zt%d" % b])
        if k == 0:
            scan(rr, ["rr%d" % k], "scr")
            list_out()
            tcopy(T.ir[:, 0:C].indirect(rt[:, 0:16]), T.wi[:, C:2 * C], ["wi", "rt%d" % k], ["ir"])
            quant_z()
            scan(T.ir, ["ir"])
            table(it[:], 0.25, ["it%d" % k])
        else:
            tcopy(T.ir[:, 0:C].indirect(T.at[:, 0:16]), T.wi[:, C:2 * C], ["wi", "at"], ["ir"])
            quant_z()
            hop(T.iv, "iv", T.ir[:, 0:C], ["ir"], T["it%d" % (k - 1)], "it%d" % (k - 1), 0, 12)
            list_row()
            scan(T.iv, ["iv.v", "iv.s"])
            table(it[:], 0.25, ["it%d" % k])
            if k < 2:
                scan(rr, ["rr%d" % k], "scr")
        cuts = ((0, 0, 128, T.psb[:, 0:128], "psb0"), (0, 128, C, T.psa[:, 0:128], "psa0")) + tuple(
            (b, 0, C, T.psb[:, 512 * b:512 * b + C], "psb%d" % b) for b in (1, 2, 3))
        for b, lo, hi, o, n in cuts:
            mm(o, T.wq[:, 128 * b:128 * b + 128], T.wp[:, 128 * b:128 * b + 128], T.qz[:, lo:hi], T.pz[:, lo:hi], True, True,
               ["wq", "wp"] + ["qz%d" % h for h in range(2) if lo <= 128 * h < hi], [n])
        for b, lo, hi, o, n in cuts:
            if k == 0 and b > 1:
                half(b)
            act(T.pb[:, C * b + lo:C * b + hi], o, [n], ["pb%d.%d" % (b, lo)], 0.015625)
        xn = T["xt%d" % (k + 1)]
        for b in range(4):
            ttt(xn[:, b:1024:4], T.pb[:, C * b:C * b + C].indirect(it[:, 0:16]), T.fh[:, C * b:C * b + C], A.add,
                ["pb%d.%d" % (c, lo) for c, lo, hi, o, n in cuts if c == b] + ["it%d" % k, "fh%d" % b], ["xt%d.%d" % (k + 1, b)])
            if b == 0 and k == 1:
                list_out()
    act(T.lnf[:], T.rr2[:], ["rr2"], ["lnf"])
    op("y", lambda: g.sync.dma_start(T.ln[:], T.lnf[0:128:16, :]), ["lnf"], ["ln"], "out", 16)
    Q3 = ["qx3.0", "qx3.1"]
    for h in range(2):
        c = 128 * h
        quant(T.qx3[:, c:c + 128], T.px3[:, c:c + 128], T.xt3[:, 4 * c:4 * c + 512], ["xt3.%d" % b for b in range(4)], [Q3[h]])
        mm(T.psa[:, 4 * c:4 * c + 128], T.vq[:, 0:128], T.vp[:, 0:128], T.qx3[:, c:c + 128], T.px3[:, c:c + 128], True, True, ["vq", Q3[h]], ["psa%d" % h])
    op("y", lambda: g.sync.dma_start(T.oc[:, 0:4 * C], T.qx3[:, 0:C].bitcast(dt.uint8)), Q3, ["oc"], "out", 16)

    def scales(q, queue, i):
        op(q, lambda: queue.dma_start(T.osc[4 * i:4 * i + 4, 0:C], T.px3[32 * i:32 * i + 4, 0:C]), Q3, ["osc%d" % i], "out", 16)

    scales("y", g.sync, 0)
    scales("y", g.sync, 1)
    tcopy(T.yb[:, 0:128], T.psa[:, 0:128], ["psa0"], ["y0"])
    act(T.yb[:, 128:C], T.psa[:, 512:640], ["psa1"], ["y1"])
    op("y", lambda: g.sync.dma_start(T.y[:, 0:128], T.yb[:, 0:128]), ["y0"], ["yo0"], "out", 16)
    op("s", lambda: S.dma_start(T.y[:, 128:C], T.yb[:, 128:C]), ["y1"], ["yo1"], "out", 16)
    scales("s", S, 2)
    scales("s", S, 3)
    for s, n in sorted(total.items()):
        g.wait_ge(T.sem[s], n)
